import numpy as np
import ml_dtypes


def mxq(x, axis, fmt="e4m3"):
    dtype, down = {"e4m3": (ml_dtypes.float8_e4m3fn, 7), "e5m2": (ml_dtypes.float8_e5m2, 14)}[fmt]
    v = np.moveaxis(np.asarray(x, np.float32).astype(ml_dtypes.bfloat16).astype(np.float64), axis, -1)
    blocks = v.reshape(v.shape[:-1] + (-1, 32))
    amax = np.abs(blocks).max(-1, keepdims=True)
    byte = np.maximum(np.where(amax > 0, np.frexp(amax)[1] - 1 + 127, 0) - down, 1)
    scale = np.exp2(byte - 127.0)
    codes = (blocks / scale).astype(np.float32).astype(dtype).astype(np.float64)
    return np.moveaxis((codes * scale).reshape(v.shape), -1, axis)


WIDE = False


def mx_kscale(k):
    if not WIDE:
        return np.ones(k)
    levels = np.array([10, -10, 5, -5, 0])
    if k % 512:
        return np.exp2(np.random.permutation(np.resize(levels, k // 32))).repeat(32)
    a = np.empty((k // 512, 16))
    for p in range(k // 512):
        a[p, :8] = np.random.permutation(np.resize(levels, 8))
        for g in range(8):
            far = levels[np.abs(levels - a[p, g]) >= 10]
            a[p, g + 8] = far[np.random.randint(len(far))]
    return np.exp2(a.ravel()).repeat(32)


def f64(x):
    return np.asarray(x).astype(np.float64)


def striped(idx):
    return np.tile(idx.reshape(-1, 16).T, (8, 1)).astype(np.uint16)


def unstriped(offs):
    return offs[:16].T.reshape(-1).astype(np.int64)


E2M1 = np.array([0.0, 0.5, 1.0, 1.5, 2.0, 3.0, 4.0, 6.0, -0.0, -0.5, -1.0, -1.5, -2.0, -3.0, -4.0, -6.0])


def pack_fp4(w):
    k, n = w.shape
    w = f64(np.asarray(w, np.float32).astype(ml_dtypes.bfloat16)).reshape(k // 32, 32, n)
    amax = np.abs(w).max(1)
    mant, ex = np.frexp(amax / 6.0)
    byte = np.clip(np.where(amax > 0, np.where(mant > 0.5, ex, ex - 1) + 127, 1), 1, 254)
    scaled = (w * np.exp2(127.0 - byte)[:, None, :]).reshape(k, n).astype(np.float32)
    c = np.ascontiguousarray(scaled.reshape(k // 512, 128, 4, n).transpose(0, 1, 3, 2)).astype(ml_dtypes.float4_e2m1fn).view(np.uint8) & 0xF
    words = (c[..., 0::2] | (c[..., 1::2] << 4)).reshape(k // 512, 128, 2 * n)
    return np.ascontiguousarray(words), np.ascontiguousarray(byte.astype(np.uint8).reshape(k // 512, 16, n))


def unpack_fp4(words, scales):
    g, _, n = scales.shape
    words = np.ascontiguousarray(words).reshape(g, 128, n, 2)
    nib = np.empty((g, 128, n, 4), np.uint8)
    nib[..., 0::2] = words & 0xF
    nib[..., 1::2] = words >> 4
    vals = E2M1[nib] * np.repeat(np.exp2(scales.astype(np.float64) - 127.0), 8, axis=1)[..., None]
    return vals.transpose(0, 1, 3, 2).reshape(g * 512, n)


def relu(v):
    return np.maximum(v, 0.0)


K, T, S, V, H, N = 512, 1024, 768, 256, 512, 128


def setup_inputs():
    n = np.random.standard_normal
    s = mx_kscale(K)[:, None]
    u = mx_kscale(H)
    packed_xT = pack_fp4(n((K, T)) * s)
    return {
        "x_words": packed_xT[0],
        "x_scales": packed_xT[1],
        "w1": (n((K, H)) / np.sqrt(K) / s * u).astype(np.float32),
        "w2": (n((K, H)) / np.sqrt(K) / s).astype(np.float32),
        "w3": (n((K, H)) / np.sqrt(K) / s).astype(np.float32),
        "w4": (n((H, N)) / np.sqrt(H) / u[:, None]).astype(np.float32),
        "offs": striped(np.random.permutation(T)[:S]),
    }


def reference(x_words, x_scales, w1, w2, w3, w4, offs):
    xq = unpack_fp4(x_words, x_scales)[:, unstriped(offs)]
    z = (((mxq(f64(w1), 0, "e4m3").T @ xq[:, :V])) * ((mxq(f64(w2), 0, "e4m3").T @ xq[:, V:2 * V]))) * ((mxq(f64(w3), 0, "e4m3").T @ xq[:, 2 * V:3 * V]))
    return relu(mxq(f64(w4), 0, "e4m3").T @ mxq(z, 0, "e4m3"))

@@ -1,0 +1,170 @@
+from contextlib import ExitStack
+
+import concourse.mybir as mybir
+
+K, T, V, H, N = 512, 1024, 256, 512, 128
+FLOPS = 2 * K * H * V * 3 + 2 * H * N * V
+
+F32 = mybir.dt.float32
+BF16 = mybir.dt.bfloat16
+I32 = mybir.dt.int32
+U32 = mybir.dt.uint32
+U16 = mybir.dt.uint16
+U8 = mybir.dt.uint8
+FP8X4 = mybir.dt.float8_e4m3fn_x4
+FP4X4 = mybir.dt.float4_e2m1fn_x4
+MULT = mybir.AluOpType.mult
+ADD = mybir.AluOpType.add
+RELU = mybir.ActivationFunctionType.Relu
+P = 128
+
+
+def tile_picked_trilin_relu_p_kernel(tc, x_words, x_scales, w1, w2, w3, w4, offs, out):
+    nc = tc.nc
+    with ExitStack() as ctx:
+        keep = ctx.enter_context(tc.tile_pool(name="keep", bufs=1))
+        psum = ctx.enter_context(tc.psum_pool(name="psum", bufs=1))
+
+        scale_table = keep.tile([P, T], U8, name="scale_table", align_bytes=64)
+        nc.vector.memset(scale_table[:].bitcast(I32), 0)
+        word_table = keep.tile([P, T], U16, name="word_table", align_bytes=64)
+        nc.sync.dma_start(word_table[:].bitcast(I32), x_words[0].bitcast(I32))
+        offsets = keep.tile([P, 48], U16, name="offsets")
+        nc.sync.dma_start(offsets[:], offs)
+        for q in range(4):
+            nc.scalar.dma_start(scale_table[32 * q : 32 * q + 4, :].bitcast(I32), x_scales[0, 4 * q : 4 * q + 4, :].bitcast(I32))
+        warm_in = keep.tile([P, 1], F32, name="warm_in")
+        warm_out = keep.tile([P, 1], F32, name="warm_out")
+        nc.gpsimd.memset(warm_in[:], 0.0)
+        nc.scalar.activation(warm_out[:], warm_in[:], RELU)
+
+        raw = {}
+        for d, w in enumerate((w1, w2, w3)):
+            rows = w.rearrange("(p j) c -> p j c", j=4)
+            for h in range(2):
+                raw[d, h] = keep.tile([P, 4, 256], F32, name="raw%d%d" % (d, h), tag="raw%d%d" % (d, h), align_bytes=64)
+                nc.sync.dma_start(raw[d, h][:], rows[:, :, 256 * h : 256 * (h + 1)])
+        raw4 = keep.tile([P, 4, N], F32, name="raw4", align_bytes=64)
+        nc.sync.dma_start(raw4[:], w4.rearrange("(p j) c -> p j c", j=4))
+
+        words01 = keep.tile([P, 2 * V], U16, name="words01", align_bytes=64)
+        words2 = keep.tile([P, V], U16, name="words2", align_bytes=64)
+        picked_scales = keep.tile([P, 3 * V], U8, name="picked_scales", align_bytes=64)
+        nc.vector.tensor_copy(words01[:], word_table[:].indirect(offsets[:, 0:32]))
+        nc.vector.tensor_copy(words2[:], word_table[:].indirect(offsets[:, 32:48]))
+        nc.vector.tensor_copy(picked_scales[:], scale_table[:].indirect(offsets[:]))
+        x_codes = [words01[:, 0:V], words01[:, V : 2 * V], words2[:]]
+        x_sc = [picked_scales[:, V * d : V * (d + 1)] for d in range(3)]
+
+        w_codes = [keep.tile([P, H], U32, name="w_codes%d" % d, align_bytes=64) for d in range(3)]
+        w_sc = [keep.tile([P, H], U8, name="w_sc%d" % d, align_bytes=64) for d in range(3)]
+        banks = {(d, h): psum.tile([P, 4, 128], F32, name="bank%d%d" % (d, h)) for d in range(3) for h in range(2)}
+        g = {}
+        p1 = {}
+        p12 = [keep.tile([P, 128, 4], F32, name="p12_%d" % h) for h in range(2)]
+        w4_codes = keep.tile([P, N], U32, name="w4_codes", align_bytes=64)
+        w4_sc = keep.tile([P, N], U8, name="w4_sc", align_bytes=64)
+        z = [keep.tile([P, 128, 4], BF16, name="z%d" % h, align_bytes=64) for h in range(2)]
+        z_codes = [keep.tile([P, 128], U32, name="z_codes%d" % h, align_bytes=64) for h in range(2)]
+        z_sc = [keep.tile([P, 128], U8, name="z_sc%d" % h, align_bytes=64) for h in range(2)]
+        acc = [psum.tile([P, 128], F32, name="acc%d" % h) for h in range(2)]
+        res = [keep.tile([P, 128], F32, name="res%d" % h) for h in range(2)]
+
+        def pool_copy(dst, src):
+            nc.gpsimd.tensor_scalar(dst, src, 1.0, 0.0, MULT, ADD)
+
+        def woven(d, h):
+            if d == 0:
+                if "first" not in g:
+                    g["first"] = keep.tile([P, 4, 128, 4], BF16, name="g0", tag="chain_a", align_bytes=64)
+                return g["first"][:, :, 64 * h : 64 * (h + 1), :]
+            if (d, h) not in g:
+                g[d, h] = keep.tile([P, 4, 64, 4], BF16, name="g%d%d" % (d, h), tag="chain_a" if h else "chain_b", align_bytes=64)
+            return g[d, h][:]
+
+        def weave(copy, d, h, m0, m1):
+            dst = woven(d, h)[:, :, m0:m1, :]
+            copy(dst.rearrange("p t m j -> p m j t"), raw[d, h][:, :, 4 * m0 : 4 * m1].rearrange("p j (m t) -> p m j t", t=4))
+
+        def quant_first():
+            nc.vector.quantize_mx(w_codes[0][:].bitcast(FP8X4), w_sc[0][:], g["first"][:].rearrange("p t m j -> p (t m j)"))
+
+        def quant(d, h):
+            for t in range(4):
+                c0 = 128 * t + 64 * h
+                nc.vector.quantize_mx(
+                    w_codes[d][:, c0 : c0 + 64].bitcast(FP8X4), w_sc[d][:, c0 : c0 + 64], g[d, h][:, t].rearrange("p m j -> p (m j)")
+                )
+
+        def products(d):
+            for h in range(2):
+                for t in range(4):
+                    nc.tensor.matmul_mx(
+                        banks[d, h][:, t, :],
+                        lhsT=w_codes[d][:, 128 * t : 128 * (t + 1)].bitcast(FP8X4),
+                        lhsT_scale=w_sc[d][:, 128 * t : 128 * (t + 1)],
+                        rhs=x_codes[d][:, 128 * h : 128 * (h + 1)].bitcast(FP4X4),
+                        rhs_scale=x_sc[d][:, 128 * h : 128 * (h + 1)],
+                        start=True,
+                        stop=True,
+                    )
+
+        def first(h):
+            p1[h] = keep.tile([P, 128, 4], F32, name="p1_%d" % h, tag="raw%d1" % (1 + h), align_bytes=64)
+            nc.scalar.copy(p1[h][:], banks[0, h][:].rearrange("p t v -> p v t"))
+
+        def second(h):
+            nc.vector.tensor_tensor(p12[h][:], banks[1, h][:].rearrange("p t v -> p v t"), p1[h][:], MULT)
+
+        def third(h):
+            nc.vector.tensor_tensor(z[h][:], banks[2, h][:].rearrange("p t v -> p v t"), p12[h][:], MULT)
+
+        def weave4():
+            g[3] = keep.tile([P, N, 4], BF16, name="g4", tag="chain_a", align_bytes=64)
+            nc.scalar.copy(g[3][:], raw4[:].rearrange("p j n -> p n j"))
+
+        def quant4():
+            nc.vector.quantize_mx(w4_codes[:].bitcast(FP8X4), w4_sc[:], g[3][:].rearrange("p n j -> p (n j)"))
+
+        def last(h):
+            nc.vector.quantize_mx(z_codes[h][:].bitcast(FP8X4), z_sc[h][:], z[h][:].rearrange("p v t -> p (v t)"))
+            nc.tensor.matmul_mx(
+                acc[h][:],
+                lhsT=w4_codes[:].bitcast(FP8X4),
+                lhsT_scale=w4_sc[:],
+                rhs=z_codes[h][:].bitcast(FP8X4),
+                rhs_scale=z_sc[h][:],
+                start=True,
+                stop=True,
+            )
+            nc.scalar.activation(res[h][:], acc[h][:], RELU)
+            nc.sync.dma_start(out[:, 128 * h : 128 * (h + 1)], res[h][:])
+
+        on_scalar, on_vector = nc.scalar.copy, nc.vector.tensor_copy
+        weave(on_scalar, 0, 0, 0, 64)
+        weave(on_scalar, 0, 1, 0, 64)
+        quant_first()
+        products(0)
+        weave(on_scalar, 1, 0, 0, 64)
+        quant(1, 0)
+        weave(on_scalar, 1, 1, 0, 32)
+        weave(on_vector, 1, 1, 32, 64)
+        quant(1, 1)
+        products(1)
+        first(0)
+        weave(on_scalar, 2, 0, 0, 32)
+        weave(on_vector, 2, 0, 32, 64)
+        weave(on_scalar, 2, 1, 0, 32)
+        weave(on_vector, 2, 1, 32, 64)
+        quant(2, 0)
+        quant(2, 1)
+        products(2)
+        second(0)
+        first(1)
+        weave4()
+        third(0)
+        second(1)
+        quant4()
+        third(1)
+        last(0)
+        last(1)

@@ -27,41 +27,40 @@ def tile_picked_trilin_relu_p_kernel(tc, x_words, x_scales, w1, w2, w3, w4, offs
 
         scale_table = keep.tile([P, T], U8, name="scale_table", align_bytes=64)
         nc.vector.memset(scale_table[:].bitcast(I32), 0)
+        scale_rows = keep.tile([P, T // 4], I32, name="scale_rows", align_bytes=64)
         word_table = keep.tile([P, T], U16, name="word_table", align_bytes=64)
-        nc.sync.dma_start(word_table[:].bitcast(I32), x_words[0].bitcast(I32))
         offsets = keep.tile([P, 48], U16, name="offsets")
-        nc.sync.dma_start(offsets[:], offs)
         for q in range(4):
-            nc.scalar.dma_start(scale_table[32 * q : 32 * q + 4, :].bitcast(I32), x_scales[0, 4 * q : 4 * q + 4, :].bitcast(I32))
+            (nc.sync, nc.scalar)[q % 2].dma_start(scale_rows[32 * q : 32 * q + 4, :], x_scales[0, 4 * q : 4 * q + 4, :].bitcast(I32))
+        nc.sync.dma_start(offsets[:], offs)
+        nc.scalar.dma_start(word_table[:].bitcast(I32), x_words[0].bitcast(I32))
+        for q in range(4):
+            nc.vector.tensor_copy(scale_table[32 * q : 32 * q + 4, :].bitcast(I32), scale_rows[32 * q : 32 * q + 4, :])
         warm_in = keep.tile([P, 1], F32, name="warm_in")
         warm_out = keep.tile([P, 1], F32, name="warm_out")
         nc.gpsimd.memset(warm_in[:], 0.0)
         nc.scalar.activation(warm_out[:], warm_in[:], RELU)
 
         raw = {}
-        for d, w in enumerate((w1, w2, w3)):
-            rows = w.rearrange("(p j) c -> p j c", j=4)
-            for h in range(2):
-                raw[d, h] = keep.tile([P, 4, 256], F32, name="raw%d%d" % (d, h), tag="raw%d%d" % (d, h), align_bytes=64)
-                nc.sync.dma_start(raw[d, h][:], rows[:, :, 256 * h : 256 * (h + 1)])
+        for name, w, c0, c1 in (("w1", w1, 0, H), ("w2", w2, 0, H), ("w3a", w3, 0, H // 2), ("w3b", w3, H // 2, H)):
+            raw[name] = keep.tile([P, 4, c1 - c0], F32, name="raw_" + name, tag="raw_" + name, align_bytes=64)
+            nc.sync.dma_start(raw[name][:], w.rearrange("(p j) c -> p j c", j=4)[:, :, c0:c1])
         raw4 = keep.tile([P, 4, N], F32, name="raw4", align_bytes=64)
-        nc.sync.dma_start(raw4[:], w4.rearrange("(p j) c -> p j c", j=4))
+        for r in range(4):
+            nc.sync.dma_start(raw4[r:P:4, :, :], w4.rearrange("(q t r) n -> r q t n", t=4, r=4)[r])
 
         words01 = keep.tile([P, 2 * V], U16, name="words01", align_bytes=64)
         words2 = keep.tile([P, V], U16, name="words2", align_bytes=64)
         picked_scales = keep.tile([P, 3 * V], U8, name="picked_scales", align_bytes=64)
+        nc.vector.tensor_copy(picked_scales[:], scale_table[:].indirect(offsets[:]))
         nc.vector.tensor_copy(words01[:], word_table[:].indirect(offsets[:, 0:32]))
         nc.vector.tensor_copy(words2[:], word_table[:].indirect(offsets[:, 32:48]))
-        nc.vector.tensor_copy(picked_scales[:], scale_table[:].indirect(offsets[:]))
         x_codes = [words01[:, 0:V], words01[:, V : 2 * V], words2[:]]
         x_sc = [picked_scales[:, V * d : V * (d + 1)] for d in range(3)]
 
         w_codes = [keep.tile([P, H], U32, name="w_codes%d" % d, align_bytes=64) for d in range(3)]
         w_sc = [keep.tile([P, H], U8, name="w_sc%d" % d, align_bytes=64) for d in range(3)]
         banks = {(d, h): psum.tile([P, 4, 128], F32, name="bank%d%d" % (d, h)) for d in range(3) for h in range(2)}
-        g = {}
-        p1 = {}
-        p12 = [keep.tile([P, 128, 4], F32, name="p12_%d" % h) for h in range(2)]
         w4_codes = keep.tile([P, N], U32, name="w4_codes", align_bytes=64)
         w4_sc = keep.tile([P, N], U8, name="w4_sc", align_bytes=64)
         z = [keep.tile([P, 128, 4], BF16, name="z%d" % h, align_bytes=64) for h in range(2)]
@@ -69,36 +68,42 @@ def tile_picked_trilin_relu_p_kernel(tc, x_words, x_scales, w1, w2, w3, w4, offs
         z_sc = [keep.tile([P, 128], U8, name="z_sc%d" % h, align_bytes=64) for h in range(2)]
         acc = [psum.tile([P, 128], F32, name="acc%d" % h) for h in range(2)]
         res = [keep.tile([P, 128], F32, name="res%d" % h) for h in range(2)]
+        g = {}
+        held = {}
 
         def pool_copy(dst, src):
             nc.gpsimd.tensor_scalar(dst, src, 1.0, 0.0, MULT, ADD)
 
-        def woven(d, h):
-            if d == 0:
-                if "first" not in g:
-                    g["first"] = keep.tile([P, 4, 128, 4], BF16, name="g0", tag="chain_a", align_bytes=64)
-                return g["first"][:, :, 64 * h : 64 * (h + 1), :]
-            if (d, h) not in g:
-                g[d, h] = keep.tile([P, 4, 64, 4], BF16, name="g%d%d" % (d, h), tag="chain_a" if h else "chain_b", align_bytes=64)
-            return g[d, h][:]
+        def woven(name, pair, tag):
+            g[name, pair] = keep.tile([P, 2, raw[name].shape[2] // 16, 4, 4], BF16, name="woven_%s_%d" % (name, pair), tag=tag, align_bytes=64)
 
-        def weave(copy, d, h, m0, m1):
-            dst = woven(d, h)[:, :, m0:m1, :]
-            copy(dst.rearrange("p t m j -> p m j t"), raw[d, h][:, :, 4 * m0 : 4 * m1].rearrange("p j (m t) -> p m j t", t=4))
+        def weave(copy, name, t0, t1, q0=0, q1=None):
+            q1 = raw[name].shape[2] // 16 if q1 is None else q1
+            src = raw[name][:].rearrange("p j (q t r) -> p t q r j", t=4, r=4)
+            copy(
+                g[name, t0 // 2][:, t0 % 2 : t0 % 2 + t1 - t0, q0:q1].rearrange("p t q r j -> p t q j r"),
+                src[:, t0:t1, q0:q1].rearrange("p t q r j -> p t q j r"),
+            )
 
-        def quant_first():
-            nc.vector.quantize_mx(w_codes[0][:].bitcast(FP8X4), w_sc[0][:], g["first"][:].rearrange("p t m j -> p (t m j)"))
+        def quant(d, name, t0, t1):
+            nc.vector.quantize_mx(
+                w_codes[d][:, 128 * t0 : 128 * t1].bitcast(FP8X4),
+                w_sc[d][:, 128 * t0 : 128 * t1],
+                g[name, t0 // 2][:, t0 % 2 : t0 % 2 + t1 - t0].rearrange("p t q r j -> p (t q r j)"),
+            )
 
-        def quant(d, h):
-            for t in range(4):
+        def quant_half(d, name, h, pair):
+            for t in range(2 * pair, 2 * pair + 2):
                 c0 = 128 * t + 64 * h
                 nc.vector.quantize_mx(
-                    w_codes[d][:, c0 : c0 + 64].bitcast(FP8X4), w_sc[d][:, c0 : c0 + 64], g[d, h][:, t].rearrange("p m j -> p (m j)")
+                    w_codes[d][:, c0 : c0 + 64].bitcast(FP8X4),
+                    w_sc[d][:, c0 : c0 + 64],
+                    g[name, pair][:, t % 2].rearrange("p q r j -> p (q r j)"),
                 )
 
-        def products(d):
+        def products(d, order):
             for h in range(2):
-                for t in range(4):
+                for t in order:
                     nc.tensor.matmul_mx(
                         banks[d, h][:, t, :],
                         lhsT=w_codes[d][:, 128 * t : 128 * (t + 1)].bitcast(FP8X4),
@@ -110,21 +115,22 @@ def tile_picked_trilin_relu_p_kernel(tc, x_words, x_scales, w1, w2, w3, w4, offs
                     )
 
         def first(h):
-            p1[h] = keep.tile([P, 128, 4], F32, name="p1_%d" % h, tag="raw%d1" % (1 + h), align_bytes=64)
-            nc.scalar.copy(p1[h][:], banks[0, h][:].rearrange("p t v -> p v t"))
+            held["p1", h] = keep.tile([P, 128, 4], F32, name="p1_%d" % h, tag=("raw_w2", "raw_w3a")[h], align_bytes=64)
+            nc.scalar.copy(held["p1", h][:], banks[0, h][:].rearrange("p t v -> p v t"))
 
         def second(h):
-            nc.vector.tensor_tensor(p12[h][:], banks[1, h][:].rearrange("p t v -> p v t"), p1[h][:], MULT)
+            held[h] = keep.tile([P, 128, 4], F32, name="p12_%d" % h, align_bytes=64)
+            nc.vector.tensor_tensor(held[h][:], banks[1, h][:].rearrange("p t v -> p v t"), held["p1", h][:], MULT)
 
         def third(h):
-            nc.vector.tensor_tensor(z[h][:], banks[2, h][:].rearrange("p t v -> p v t"), p12[h][:], MULT)
+            nc.vector.tensor_tensor(z[h][:], banks[2, h][:].rearrange("p t v -> p v t"), held[h][:], MULT)
 
         def weave4():
-            g[3] = keep.tile([P, N, 4], BF16, name="g4", tag="chain_a", align_bytes=64)
-            nc.scalar.copy(g[3][:], raw4[:].rearrange("p j n -> p n j"))
+            g[4] = keep.tile([P, N, 4], BF16, name="woven_w4", tag="ring_a", align_bytes=64)
+            nc.scalar.copy(g[4][:].rearrange("p (c i) t -> p c t i", i=4), raw4[:].rearrange("p t (c i) -> p c t i", i=4))
 
         def quant4():
-            nc.vector.quantize_mx(w4_codes[:].bitcast(FP8X4), w4_sc[:], g[3][:].rearrange("p n j -> p (n j)"))
+            nc.vector.quantize_mx(w4_codes[:].bitcast(FP8X4), w4_sc[:], g[4][:].rearrange("p n t -> p (n t)"))
 
         def last(h):
             nc.vector.quantize_mx(z_codes[h][:].bitcast(FP8X4), z_sc[h][:], z[h][:].rearrange("p v t -> p (v t)"))
@@ -138,32 +144,45 @@ def tile_picked_trilin_relu_p_kernel(tc, x_words, x_scales, w1, w2, w3, w4, offs
                 stop=True,
             )
             nc.scalar.activation(res[h][:], acc[h][:], RELU)
-            nc.sync.dma_start(out[:, 128 * h : 128 * (h + 1)], res[h][:])
+            (nc.sync, nc.scalar)[h].dma_start(out[:, 128 * h : 128 * (h + 1)], res[h][:])
 
         on_scalar, on_vector = nc.scalar.copy, nc.vector.tensor_copy
-        weave(on_scalar, 0, 0, 0, 64)
-        weave(on_scalar, 0, 1, 0, 64)
-        quant_first()
-        products(0)
-        weave(on_scalar, 1, 0, 0, 64)
-        quant(1, 0)
-        weave(on_scalar, 1, 1, 0, 32)
-        weave(on_vector, 1, 1, 32, 64)
-        quant(1, 1)
-        products(1)
+        woven("w1", 0, "ring_a")
+        woven("w1", 1, "ring_c")
+        weave(on_scalar, "w1", 2, 4)
+        weave(on_scalar, "w1", 1, 2)
+        weave(on_vector, "w1", 0, 1)
+        quant(0, "w1", 2, 4)
+        quant(0, "w1", 0, 2)
+        products(0, (2, 3, 0, 1))
+        woven("w2", 0, "ring_a")
+        woven("w2", 1, "ring_b")
+        weave(on_scalar, "w2", 2, 4)
+        weave(on_vector, "w2", 0, 1)
+        weave(on_vector, "w2", 1, 2)
+        quant(1, "w2", 0, 1)
+        quant(1, "w2", 1, 2)
+        quant(1, "w2", 2, 4)
+        products(1, (0, 1, 2, 3))
         first(0)
-        weave(on_scalar, 2, 0, 0, 32)
-        weave(on_vector, 2, 0, 32, 64)
-        weave(on_scalar, 2, 1, 0, 32)
-        weave(on_vector, 2, 1, 32, 64)
-        quant(2, 0)
-        quant(2, 1)
-        products(2)
+        woven("w3a", 0, "ring_b")
+        woven("w3a", 1, "ring_c")
+        weave(on_scalar, "w3a", 2, 4)
+        weave(on_vector, "w3a", 0, 2)
         second(0)
+        quant_half(2, "w3a", 0, 0)
+        quant_half(2, "w3a", 0, 1)
+        woven("w3b", 0, "ring_b")
+        woven("w3b", 1, "ring_a")
+        weave(on_scalar, "w3b", 2, 4)
+        weave(on_vector, "w3b", 0, 2)
+        quant_half(2, "w3b", 1, 0)
+        quant_half(2, "w3b", 1, 1)
+        products(2, (0, 1, 2, 3))
         first(1)
+        second(1)
         weave4()
         third(0)
-        second(1)
         quant4()
         third(1)
         last(0)

@@ -42,7 +42,7 @@ def tile_picked_trilin_relu_p_kernel(tc, x_words, x_scales, w1, w2, w3, w4, offs
         nc.scalar.activation(warm_out[:], warm_in[:], RELU)
 
         raw = {}
-        for name, w, c0, c1 in (("w1", w1, 0, H), ("w2", w2, 0, H), ("w3a", w3, 0, H // 2), ("w3b", w3, H // 2, H)):
+        for name, w, c0, c1 in [("w%d%s" % (d + 1, ("a", "b")[h]), w, 256 * h, 256 * (h + 1)) for d, w in enumerate((w1, w2, w3)) for h in range(2)]:
             raw[name] = keep.tile([P, 4, c1 - c0], F32, name="raw_" + name, tag="raw_" + name, align_bytes=64)
             nc.sync.dma_start(raw[name][:], w.rearrange("(p j) c -> p j c", j=4)[:, :, c0:c1])
         raw4 = keep.tile([P, 4, N], F32, name="raw4", align_bytes=64)
@@ -74,16 +74,17 @@ def tile_picked_trilin_relu_p_kernel(tc, x_words, x_scales, w1, w2, w3, w4, offs
         def pool_copy(dst, src):
             nc.gpsimd.tensor_scalar(dst, src, 1.0, 0.0, MULT, ADD)
 
-        def woven(name, pair, tag):
-            g[name, pair] = keep.tile([P, 2, raw[name].shape[2] // 16, 4, 4], BF16, name="woven_%s_%d" % (name, pair), tag=tag, align_bytes=64)
+        def woven(name, pair, tag, groups):
+            g[name, pair] = keep.tile([P, 2, groups, 4, 4], BF16, name="woven_%s_%d" % (name, pair), tag=tag, align_bytes=64)
 
-        def weave(copy, name, t0, t1, q0=0, q1=None):
-            q1 = raw[name].shape[2] // 16 if q1 is None else q1
-            src = raw[name][:].rearrange("p j (q t r) -> p t q r j", t=4, r=4)
-            copy(
-                g[name, t0 // 2][:, t0 % 2 : t0 % 2 + t1 - t0, q0:q1].rearrange("p t q r j -> p t q j r"),
-                src[:, t0:t1, q0:q1].rearrange("p t q r j -> p t q j r"),
-            )
+        def weave(copy, chunk, name, t0, t1, q0=0):
+            src = raw[chunk][:].rearrange("p j (q t r) -> p t q r j", t=4, r=4)
+            for pair in range(t0 // 2, (t1 + 1) // 2):
+                a, b = max(t0, 2 * pair), min(t1, 2 * pair + 2)
+                copy(
+                    g[name, pair][:, a % 2 : a % 2 + b - a, q0 : q0 + 16].rearrange("p t q r j -> p t q j r"),
+                    src[:, a:b].rearrange("p t q r j -> p t q j r"),
+                )
 
         def quant(d, name, t0, t1):
             nc.vector.quantize_mx(
@@ -115,18 +116,18 @@ def tile_picked_trilin_relu_p_kernel(tc, x_words, x_scales, w1, w2, w3, w4, offs
                     )
 
         def first(h):
-            held["p1", h] = keep.tile([P, 128, 4], F32, name="p1_%d" % h, tag=("raw_w2", "raw_w3a")[h], align_bytes=64)
+            held["p1", h] = keep.tile([P, 128, 4], F32, name="p1_%d" % h, tag=("raw_w2b", "raw_w3b")[h], align_bytes=64)
             nc.scalar.copy(held["p1", h][:], banks[0, h][:].rearrange("p t v -> p v t"))
 
         def second(h):
-            held[h] = keep.tile([P, 128, 4], F32, name="p12_%d" % h, align_bytes=64)
+            held[h] = keep.tile([P, 128, 4], F32, name="p12_%d" % h, tag=("p12_a", "w3_hi")[h], align_bytes=64)
             nc.vector.tensor_tensor(held[h][:], banks[1, h][:].rearrange("p t v -> p v t"), held["p1", h][:], MULT)
 
         def third(h):
             nc.vector.tensor_tensor(z[h][:], banks[2, h][:].rearrange("p t v -> p v t"), held[h][:], MULT)
 
         def weave4():
-            g[4] = keep.tile([P, N, 4], BF16, name="woven_w4", tag="ring_a", align_bytes=64)
+            g[4] = keep.tile([P, N, 4], BF16, name="woven_w4", tag="w2_hi", align_bytes=64)
             nc.scalar.copy(g[4][:].rearrange("p (c i) t -> p c t i", i=4), raw4[:].rearrange("p t (c i) -> p c t i", i=4))
 
         def quant4():
@@ -147,37 +148,35 @@ def tile_picked_trilin_relu_p_kernel(tc, x_words, x_scales, w1, w2, w3, w4, offs
             (nc.sync, nc.scalar)[h].dma_start(out[:, 128 * h : 128 * (h + 1)], res[h][:])
 
         on_scalar, on_vector = nc.scalar.copy, nc.vector.tensor_copy
-        woven("w1", 0, "ring_a")
-        woven("w1", 1, "ring_c")
-        weave(on_scalar, "w1", 2, 4)
-        weave(on_scalar, "w1", 1, 2)
-        weave(on_vector, "w1", 0, 1)
-        quant(0, "w1", 2, 4)
+        for name in ("w1", "w2"):
+            woven(name, 0, name + "_lo", 32)
+            woven(name, 1, name + "_hi", 32)
+        weave(on_scalar, "w1a", "w1", 0, 4)
+        weave(on_scalar, "w1b", "w1", 0, 4, 16)
         quant(0, "w1", 0, 2)
-        products(0, (2, 3, 0, 1))
-        woven("w2", 0, "ring_a")
-        woven("w2", 1, "ring_b")
-        weave(on_scalar, "w2", 2, 4)
-        weave(on_vector, "w2", 0, 1)
-        weave(on_vector, "w2", 1, 2)
+        quant(0, "w1", 2, 4)
+        products(0, (0, 1, 2, 3))
+        weave(on_scalar, "w2a", "w2", 1, 4)
+        weave(on_vector, "w2a", "w2", 0, 1)
+        weave(on_scalar, "w2b", "w2", 2, 4, 16)
+        weave(on_vector, "w2b", "w2", 0, 1, 16)
+        weave(on_vector, "w2b", "w2", 1, 2, 16)
         quant(1, "w2", 0, 1)
         quant(1, "w2", 1, 2)
         quant(1, "w2", 2, 4)
         products(1, (0, 1, 2, 3))
         first(0)
-        woven("w3a", 0, "ring_b")
-        woven("w3a", 1, "ring_c")
-        weave(on_scalar, "w3a", 2, 4)
-        weave(on_vector, "w3a", 0, 2)
+        woven("w3", 0, "w2_hi", 32)
+        woven("w3", 1, "w3_hi", 32)
+        weave(on_scalar, "w3a", "w3", 2, 4)
+        weave(on_vector, "w3a", "w3", 0, 2)
         second(0)
-        quant_half(2, "w3a", 0, 0)
-        quant_half(2, "w3a", 0, 1)
-        woven("w3b", 0, "ring_b")
-        woven("w3b", 1, "ring_a")
-        weave(on_scalar, "w3b", 2, 4)
-        weave(on_vector, "w3b", 0, 2)
-        quant_half(2, "w3b", 1, 0)
-        quant_half(2, "w3b", 1, 1)
+        weave(on_scalar, "w3b", "w3", 2, 4, 16)
+        weave(on_vector, "w3b", "w3", 0, 1, 16)
+        weave(on_vector, "w3b", "w3", 1, 2, 16)
+        quant(2, "w3", 0, 1)
+        quant(2, "w3", 1, 2)
+        quant(2, "w3", 2, 4)
         products(2, (0, 1, 2, 3))
         first(1)
         second(1)

@@ -14,7 +14,6 @@ U8 = mybir.dt.uint8
 FP8X4 = mybir.dt.float8_e4m3fn_x4
 FP4X4 = mybir.dt.float4_e2m1fn_x4
 MULT = mybir.AluOpType.mult
-ADD = mybir.AluOpType.add
 RELU = mybir.ActivationFunctionType.Relu
 P = 128
 
@@ -71,9 +70,6 @@ def tile_picked_trilin_relu_p_kernel(tc, x_words, x_scales, w1, w2, w3, w4, offs
         g = {}
         held = {}
 
-        def pool_copy(dst, src):
-            nc.gpsimd.tensor_scalar(dst, src, 1.0, 0.0, MULT, ADD)
-
         def woven(name, pair, tag, groups):
             g[name, pair] = keep.tile([P, 2, groups, 4, 4], BF16, name="woven_%s_%d" % (name, pair), tag=tag, align_bytes=64)
 
@@ -93,15 +89,6 @@ def tile_picked_trilin_relu_p_kernel(tc, x_words, x_scales, w1, w2, w3, w4, offs
                 g[name, t0 // 2][:, t0 % 2 : t0 % 2 + t1 - t0].rearrange("p t q r j -> p (t q r j)"),
             )
 
-        def quant_half(d, name, h, pair):
-            for t in range(2 * pair, 2 * pair + 2):
-                c0 = 128 * t + 64 * h
-                nc.vector.quantize_mx(
-                    w_codes[d][:, c0 : c0 + 64].bitcast(FP8X4),
-                    w_sc[d][:, c0 : c0 + 64],
-                    g[name, pair][:, t % 2].rearrange("p q r j -> p (q r j)"),
-                )
-
         def products(d, order):
             for h in range(2):
                 for t in order:
@@ -116,12 +103,11 @@ def tile_picked_trilin_relu_p_kernel(tc, x_words, x_scales, w1, w2, w3, w4, offs
                     )
 
         def first(h):
-            held["p1", h] = keep.tile([P, 128, 4], F32, name="p1_%d" % h, tag=("raw_w2b", "raw_w3b")[h], align_bytes=64)
-            nc.scalar.copy(held["p1", h][:], banks[0, h][:].rearrange("p t v -> p v t"))
+            nc.scalar.copy(p1_both[:, h], banks[0, h][:].rearrange("p t v -> p v t"))
 
         def second(h):
             held[h] = keep.tile([P, 128, 4], F32, name="p12_%d" % h, tag=("p12_a", "w3_hi")[h], align_bytes=64)
-            nc.vector.tensor_tensor(held[h][:], banks[1, h][:].rearrange("p t v -> p v t"), held["p1", h][:], MULT)
+            nc.vector.tensor_tensor(held[h][:], banks[1, h][:].rearrange("p t v -> p v t"), p1_both[:, h], MULT)
 
         def third(h):
             nc.vector.tensor_tensor(z[h][:], banks[2, h][:].rearrange("p t v -> p v t"), held[h][:], MULT)
@@ -165,7 +151,9 @@ def tile_picked_trilin_relu_p_kernel(tc, x_words, x_scales, w1, w2, w3, w4, offs
         quant(1, "w2", 1, 2)
         quant(1, "w2", 2, 4)
         products(1, (0, 1, 2, 3))
+        p1_both = keep.tile([P, 2, 128, 4], F32, name="p1_both", tag="raw_w2b", align_bytes=64)
         first(0)
+        first(1)
         woven("w3", 0, "w2_hi", 32)
         woven("w3", 1, "w3_hi", 32)
         weave(on_scalar, "w3a", "w3", 2, 4)
@@ -178,7 +166,6 @@ def tile_picked_trilin_relu_p_kernel(tc, x_words, x_scales, w1, w2, w3, w4, offs
         quant(2, "w3", 1, 2)
         quant(2, "w3", 2, 4)
         products(2, (0, 1, 2, 3))
-        first(1)
         second(1)
         weave4()
         third(0)

@@ -26,15 +26,12 @@ def tile_picked_trilin_relu_p_kernel(tc, x_words, x_scales, w1, w2, w3, w4, offs
 
         scale_table = keep.tile([P, T], U8, name="scale_table", align_bytes=64)
         nc.vector.memset(scale_table[:].bitcast(I32), 0)
-        scale_rows = keep.tile([P, T // 4], I32, name="scale_rows", align_bytes=64)
         word_table = keep.tile([P, T], U16, name="word_table", align_bytes=64)
         offsets = keep.tile([P, 48], U16, name="offsets")
-        for q in range(4):
-            (nc.sync, nc.scalar)[q % 2].dma_start(scale_rows[32 * q : 32 * q + 4, :], x_scales[0, 4 * q : 4 * q + 4, :].bitcast(I32))
         nc.sync.dma_start(offsets[:], offs)
         nc.scalar.dma_start(word_table[:].bitcast(I32), x_words[0].bitcast(I32))
         for q in range(4):
-            nc.vector.tensor_copy(scale_table[32 * q : 32 * q + 4, :].bitcast(I32), scale_rows[32 * q : 32 * q + 4, :])
+            (nc.sync, nc.scalar)[q % 2].dma_start(scale_table[32 * q : 32 * q + 4, :].bitcast(I32), x_scales[0, 4 * q : 4 * q + 4, :].bitcast(I32))
         warm_in = keep.tile([P, 1], F32, name="warm_in")
         warm_out = keep.tile([P, 1], F32, name="warm_out")
         nc.gpsimd.memset(warm_in[:], 0.0)
@@ -45,15 +42,15 @@ def tile_picked_trilin_relu_p_kernel(tc, x_words, x_scales, w1, w2, w3, w4, offs
             raw[name] = keep.tile([P, 4, c1 - c0], F32, name="raw_" + name, tag="raw_" + name, align_bytes=64)
             nc.sync.dma_start(raw[name][:], w.rearrange("(p j) c -> p j c", j=4)[:, :, c0:c1])
         raw4 = keep.tile([P, 4, N], F32, name="raw4", align_bytes=64)
-        for r in range(4):
-            nc.sync.dma_start(raw4[r:P:4, :, :], w4.rearrange("(q t r) n -> r q t n", t=4, r=4)[r])
+        for r in range(2):
+            nc.sync.dma_start(raw4[r:P:2, :, :], w4.rearrange("(q t r) n -> r q t n", t=4, r=2)[r])
 
         words01 = keep.tile([P, 2 * V], U16, name="words01", align_bytes=64)
         words2 = keep.tile([P, V], U16, name="words2", align_bytes=64)
         picked_scales = keep.tile([P, 3 * V], U8, name="picked_scales", align_bytes=64)
-        nc.vector.tensor_copy(picked_scales[:], scale_table[:].indirect(offsets[:]))
         nc.vector.tensor_copy(words01[:], word_table[:].indirect(offsets[:, 0:32]))
         nc.vector.tensor_copy(words2[:], word_table[:].indirect(offsets[:, 32:48]))
+        nc.vector.tensor_copy(picked_scales[:], scale_table[:].indirect(offsets[:]))
         x_codes = [words01[:, 0:V], words01[:, V : 2 * V], words2[:]]
         x_sc = [picked_scales[:, V * d : V * (d + 1)] for d in range(3)]
 
@@ -71,15 +68,15 @@ def tile_picked_trilin_relu_p_kernel(tc, x_words, x_scales, w1, w2, w3, w4, offs
         held = {}
 
         def woven(name, pair, tag, groups):
-            g[name, pair] = keep.tile([P, 2, groups, 4, 4], BF16, name="woven_%s_%d" % (name, pair), tag=tag, align_bytes=64)
+            g[name, pair] = keep.tile([P, 2, groups, 2, 4], BF16, name="woven_%s_%d" % (name, pair), tag=tag, align_bytes=64)
 
         def weave(copy, chunk, name, t0, t1, q0=0):
-            src = raw[chunk][:].rearrange("p j (q t r) -> p t q r j", t=4, r=4)
+            src = raw[chunk][:].rearrange("p j (q t r) -> p t q r j", t=4, r=2)
             for pair in range(t0 // 2, (t1 + 1) // 2):
                 a, b = max(t0, 2 * pair), min(t1, 2 * pair + 2)
                 copy(
-                    g[name, pair][:, a % 2 : a % 2 + b - a, q0 : q0 + 16].rearrange("p t q r j -> p t q j r"),
-                    src[:, a:b].rearrange("p t q r j -> p t q j r"),
+                    g[name, pair][:, a % 2 : a % 2 + b - a, q0 : q0 + 32].rearrange("p t q r j -> p q j t r"),
+                    src[:, a:b].rearrange("p t q r j -> p q j t r"),
                 )
 
         def quant(d, name, t0, t1):
@@ -113,7 +110,7 @@ def tile_picked_trilin_relu_p_kernel(tc, x_words, x_scales, w1, w2, w3, w4, offs
             nc.vector.tensor_tensor(z[h][:], banks[2, h][:].rearrange("p t v -> p v t"), held[h][:], MULT)
 
         def weave4():
-            g[4] = keep.tile([P, N, 4], BF16, name="woven_w4", tag="w2_hi", align_bytes=64)
+            g[4] = keep.tile([P, N, 4], BF16, name="woven_w4", tag="w2_lo", align_bytes=64)
             nc.scalar.copy(g[4][:].rearrange("p (c i) t -> p c t i", i=4), raw4[:].rearrange("p t (c i) -> p c t i", i=4))
 
         def quant4():
@@ -135,18 +132,18 @@ def tile_picked_trilin_relu_p_kernel(tc, x_words, x_scales, w1, w2, w3, w4, offs
 
         on_scalar, on_vector = nc.scalar.copy, nc.vector.tensor_copy
         for name in ("w1", "w2"):
-            woven(name, 0, name + "_lo", 32)
-            woven(name, 1, name + "_hi", 32)
+            woven(name, 0, name + "_lo", 64)
+            woven(name, 1, name + "_hi", 64)
         weave(on_scalar, "w1a", "w1", 0, 4)
-        weave(on_scalar, "w1b", "w1", 0, 4, 16)
+        weave(on_scalar, "w1b", "w1", 0, 4, 32)
         quant(0, "w1", 0, 2)
         quant(0, "w1", 2, 4)
         products(0, (0, 1, 2, 3))
         weave(on_scalar, "w2a", "w2", 1, 4)
         weave(on_vector, "w2a", "w2", 0, 1)
-        weave(on_scalar, "w2b", "w2", 2, 4, 16)
-        weave(on_vector, "w2b", "w2", 0, 1, 16)
-        weave(on_vector, "w2b", "w2", 1, 2, 16)
+        weave(on_scalar, "w2b", "w2", 2, 4, 32)
+        weave(on_vector, "w2b", "w2", 0, 1, 32)
+        weave(on_vector, "w2b", "w2", 1, 2, 32)
         quant(1, "w2", 0, 1)
         quant(1, "w2", 1, 2)
         quant(1, "w2", 2, 4)
@@ -154,22 +151,22 @@ def tile_picked_trilin_relu_p_kernel(tc, x_words, x_scales, w1, w2, w3, w4, offs
         p1_both = keep.tile([P, 2, 128, 4], F32, name="p1_both", tag="raw_w2b", align_bytes=64)
         first(0)
         first(1)
-        woven("w3", 0, "w2_hi", 32)
-        woven("w3", 1, "w3_hi", 32)
+        woven("w3", 0, "w2_hi", 64)
+        woven("w3", 1, "w3_hi", 64)
         weave(on_scalar, "w3a", "w3", 2, 4)
         weave(on_vector, "w3a", "w3", 0, 2)
         second(0)
-        weave(on_scalar, "w3b", "w3", 2, 4, 16)
-        weave(on_vector, "w3b", "w3", 0, 1, 16)
-        weave(on_vector, "w3b", "w3", 1, 2, 16)
+        weave(on_scalar, "w3b", "w3", 2, 4, 32)
+        weave(on_vector, "w3b", "w3", 0, 1, 32)
+        weave(on_vector, "w3b", "w3", 1, 2, 32)
         quant(2, "w3", 0, 1)
         quant(2, "w3", 1, 2)
         quant(2, "w3", 2, 4)
         products(2, (0, 1, 2, 3))
-        second(1)
         weave4()
-        third(0)
         quant4()
+        second(1)
+        third(0)
         third(1)
         last(0)
         last(1)

@@ -75,8 +75,8 @@ def tile_picked_trilin_relu_p_kernel(tc, x_words, x_scales, w1, w2, w3, w4, offs
             for pair in range(t0 // 2, (t1 + 1) // 2):
                 a, b = max(t0, 2 * pair), min(t1, 2 * pair + 2)
                 copy(
-                    g[name, pair][:, a % 2 : a % 2 + b - a, q0 : q0 + 32].rearrange("p t q r j -> p q j t r"),
-                    src[:, a:b].rearrange("p t q r j -> p q j t r"),
+                    g[name, pair][:, a % 2 : a % 2 + b - a, q0 : q0 + 32].rearrange("p t q r j -> p t q j r"),
+                    src[:, a:b].rearrange("p t q r j -> p t q j r"),
                 )
 
         def quant(d, name, t0, t1):
@@ -111,7 +111,7 @@ def tile_picked_trilin_relu_p_kernel(tc, x_words, x_scales, w1, w2, w3, w4, offs
 
         def weave4():
             g[4] = keep.tile([P, N, 4], BF16, name="woven_w4", tag="w2_lo", align_bytes=64)
-            nc.scalar.copy(g[4][:].rearrange("p (c i) t -> p c t i", i=4), raw4[:].rearrange("p t (c i) -> p c t i", i=4))
+            nc.scalar.copy(g[4][:].rearrange("p (c i) t -> p c t i", i=2), raw4[:].rearrange("p t (c i) -> p c t i", i=2))
 
         def quant4():
             nc.vector.quantize_mx(w4_codes[:].bitcast(FP8X4), w4_sc[:], g[4][:].rearrange("p n t -> p (n t)"))

@@ -39,8 +39,8 @@ def tile_picked_trilin_relu_p_kernel(tc, x_words, x_scales, w1, w2, w3, w4, offs
 
         raw = {}
         for name, w, c0, c1 in [("w%d%s" % (d + 1, ("a", "b")[h]), w, 256 * h, 256 * (h + 1)) for d, w in enumerate((w1, w2, w3)) for h in range(2)]:
-            raw[name] = keep.tile([P, 4, c1 - c0], F32, name="raw_" + name, tag="raw_" + name, align_bytes=64)
-            nc.sync.dma_start(raw[name][:], w.rearrange("(p j) c -> p j c", j=4)[:, :, c0:c1])
+            raw[name] = keep.tile([P, 4 * (c1 - c0)], F32, name="raw_" + name, tag="raw_" + name, align_bytes=64)[:].rearrange("p (j c) -> p j c", j=4)
+            nc.sync.dma_start(raw[name], w.rearrange("(p j) c -> p j c", j=4)[:, :, c0:c1])
         raw4 = keep.tile([P, 4, N], F32, name="raw4", align_bytes=64)
         for r in range(2):
             nc.sync.dma_start(raw4[r:P:2, :, :], w4.rearrange("(q t r) n -> r q t n", t=4, r=2)[r])
@@ -56,7 +56,11 @@ def tile_picked_trilin_relu_p_kernel(tc, x_words, x_scales, w1, w2, w3, w4, offs
 
         w_codes = [keep.tile([P, H], U32, name="w_codes%d" % d, align_bytes=64) for d in range(3)]
         w_sc = [keep.tile([P, H], U8, name="w_sc%d" % d, align_bytes=64) for d in range(3)]
-        banks = {(d, h): psum.tile([P, 4, 128], F32, name="bank%d%d" % (d, h)) for d in range(3) for h in range(2)}
+        pair_banks = {(d, u): psum.tile([P, 2, V], F32, name="bank%d%d" % (d, u)) for d in range(2) for u in range(2)}
+        half_banks = [psum.tile([P, 4, 128], F32, name="bank2%d" % h) for h in range(2)]
+        p12 = keep.tile([P, 2, V, 2], F32, name="p12", align_bytes=64)
+        arena = keep.tile([P, 1792], F32, name="arena", align_bytes=64)
+        p1 = [arena[:, 512 * u : 512 * (u + 1)].rearrange("p (v e) -> p v e", e=2) for u in range(2)]
         w4_codes = keep.tile([P, N], U32, name="w4_codes", align_bytes=64)
         w4_sc = keep.tile([P, N], U8, name="w4_sc", align_bytes=64)
         z = [keep.tile([P, 128, 4], BF16, name="z%d" % h, align_bytes=64) for h in range(2)]
@@ -65,56 +69,59 @@ def tile_picked_trilin_relu_p_kernel(tc, x_words, x_scales, w1, w2, w3, w4, offs
         acc = [psum.tile([P, 128], F32, name="acc%d" % h) for h in range(2)]
         res = [keep.tile([P, 128], F32, name="res%d" % h) for h in range(2)]
         g = {}
-        held = {}
 
-        def woven(name, pair, tag, groups):
-            g[name, pair] = keep.tile([P, 2, groups, 2, 4], BF16, name="woven_%s_%d" % (name, pair), tag=tag, align_bytes=64)
+        def weave(copy, d, half, t0, t1, q0, q1):
+            src = raw["w%d%s" % (d + 1, "ab"[half])].rearrange("p j (q t r) -> p t q j r", t=4, r=2)
+            dst = g[d].rearrange("p t q r j -> p t q j r")
+            copy(dst[:, t0:t1, 32 * half + q0 : 32 * half + q1], src[:, t0:t1, q0:q1])
 
-        def weave(copy, chunk, name, t0, t1, q0=0):
-            src = raw[chunk][:].rearrange("p j (q t r) -> p t q r j", t=4, r=2)
-            for pair in range(t0 // 2, (t1 + 1) // 2):
-                a, b = max(t0, 2 * pair), min(t1, 2 * pair + 2)
-                copy(
-                    g[name, pair][:, a % 2 : a % 2 + b - a, q0 : q0 + 32].rearrange("p t q r j -> p t q j r"),
-                    src[:, a:b].rearrange("p t q r j -> p t q j r"),
-                )
-
-        def quant(d, name, t0, t1):
+        def quant(d, t0, t1):
             nc.vector.quantize_mx(
                 w_codes[d][:, 128 * t0 : 128 * t1].bitcast(FP8X4),
                 w_sc[d][:, 128 * t0 : 128 * t1],
-                g[name, t0 // 2][:, t0 % 2 : t0 % 2 + t1 - t0].rearrange("p t q r j -> p (t q r j)"),
+                g[d][:, t0:t1].rearrange("p t q r j -> p (t q r j)"),
             )
 
-        def products(d, order):
+        def product(bank, d, t, v0, v1):
+            nc.tensor.matmul_mx(
+                bank,
+                lhsT=w_codes[d][:, 128 * t : 128 * (t + 1)].bitcast(FP8X4),
+                lhsT_scale=w_sc[d][:, 128 * t : 128 * (t + 1)],
+                rhs=x_codes[d][:, v0:v1].bitcast(FP4X4),
+                rhs_scale=x_sc[d][:, v0:v1],
+                start=True,
+                stop=True,
+            )
+
+        def pair_products(d):
+            for t in range(4):
+                product(pair_banks[d, t // 2][:, t % 2, :], d, t, 0, V)
+
+        def half_products():
             for h in range(2):
-                for t in order:
-                    nc.tensor.matmul_mx(
-                        banks[d, h][:, t, :],
-                        lhsT=w_codes[d][:, 128 * t : 128 * (t + 1)].bitcast(FP8X4),
-                        lhsT_scale=w_sc[d][:, 128 * t : 128 * (t + 1)],
-                        rhs=x_codes[d][:, 128 * h : 128 * (h + 1)].bitcast(FP4X4),
-                        rhs_scale=x_sc[d][:, 128 * h : 128 * (h + 1)],
-                        start=True,
-                        stop=True,
-                    )
+                for t in range(4):
+                    product(half_banks[h][:, t, :], 2, t, 128 * h, 128 * (h + 1))
 
-        def first(h):
-            nc.scalar.copy(p1_both[:, h], banks[0, h][:].rearrange("p t v -> p v t"))
+        def first(u, v0, v1):
+            nc.scalar.copy(p1[u][:, v0:v1], pair_banks[0, u][:, :, v0:v1].rearrange("p e v -> p v e"))
 
-        def second(h):
-            held[h] = keep.tile([P, 128, 4], F32, name="p12_%d" % h, tag=("p12_a", "w3_hi")[h], align_bytes=64)
-            nc.vector.tensor_tensor(held[h][:], banks[1, h][:].rearrange("p t v -> p v t"), p1_both[:, h], MULT)
+        def second(u, v0, v1):
+            nc.vector.tensor_tensor(p12[:, u, v0:v1], pair_banks[1, u][:, :, v0:v1].rearrange("p e v -> p v e"), p1[u][:, v0:v1], MULT)
 
         def third(h):
-            nc.vector.tensor_tensor(z[h][:], banks[2, h][:].rearrange("p t v -> p v t"), held[h][:], MULT)
+            nc.vector.tensor_tensor(
+                z[h][:].rearrange("p v (u e) -> p v u e", e=2),
+                half_banks[h][:].rearrange("p (u e) v -> p v u e", e=2),
+                p12[:, :, 128 * h : 128 * (h + 1), :].rearrange("p u v e -> p v u e"),
+                MULT,
+            )
 
         def weave4():
-            g[4] = keep.tile([P, N, 4], BF16, name="woven_w4", tag="w2_lo", align_bytes=64)
-            nc.scalar.copy(g[4][:].rearrange("p (c i) t -> p c t i", i=2), raw4[:].rearrange("p t (c i) -> p c t i", i=2))
+            g["w4"] = arena[:, 1024:1280].bitcast(BF16).rearrange("p (n t) -> p n t", t=4)
+            nc.scalar.copy(g["w4"].rearrange("p (c i) t -> p c t i", i=2), raw4[:].rearrange("p t (c i) -> p c t i", i=2))
 
         def quant4():
-            nc.vector.quantize_mx(w4_codes[:].bitcast(FP8X4), w4_sc[:], g[4][:].rearrange("p n t -> p (n t)"))
+            nc.vector.quantize_mx(w4_codes[:].bitcast(FP8X4), w4_sc[:], g["w4"].rearrange("p n t -> p (n t)"))
 
         def last(h):
             nc.vector.quantize_mx(z_codes[h][:].bitcast(FP8X4), z_sc[h][:], z[h][:].rearrange("p v t -> p (v t)"))
@@ -131,42 +138,41 @@ def tile_picked_trilin_relu_p_kernel(tc, x_words, x_scales, w1, w2, w3, w4, offs
             (nc.sync, nc.scalar)[h].dma_start(out[:, 128 * h : 128 * (h + 1)], res[h][:])
 
         on_scalar, on_vector = nc.scalar.copy, nc.vector.tensor_copy
-        for name in ("w1", "w2"):
-            woven(name, 0, name + "_lo", 64)
-            woven(name, 1, name + "_hi", 64)
-        weave(on_scalar, "w1a", "w1", 0, 4)
-        weave(on_scalar, "w1b", "w1", 0, 4, 32)
-        quant(0, "w1", 0, 2)
-        quant(0, "w1", 2, 4)
-        products(0, (0, 1, 2, 3))
-        weave(on_scalar, "w2a", "w2", 1, 4)
-        weave(on_vector, "w2a", "w2", 0, 1)
-        weave(on_scalar, "w2b", "w2", 2, 4, 32)
-        weave(on_vector, "w2b", "w2", 0, 1, 32)
-        weave(on_vector, "w2b", "w2", 1, 2, 32)
-        quant(1, "w2", 0, 1)
-        quant(1, "w2", 1, 2)
-        quant(1, "w2", 2, 4)
-        products(1, (0, 1, 2, 3))
-        p1_both = keep.tile([P, 2, 128, 4], F32, name="p1_both", tag="raw_w2b", align_bytes=64)
-        first(0)
-        first(1)
-        woven("w3", 0, "w2_hi", 64)
-        woven("w3", 1, "w3_hi", 64)
-        weave(on_scalar, "w3a", "w3", 2, 4)
-        weave(on_vector, "w3a", "w3", 0, 2)
-        second(0)
-        weave(on_scalar, "w3b", "w3", 2, 4, 32)
-        weave(on_vector, "w3b", "w3", 0, 1, 32)
-        weave(on_vector, "w3b", "w3", 1, 2, 32)
-        quant(2, "w3", 0, 1)
-        quant(2, "w3", 1, 2)
-        quant(2, "w3", 2, 4)
-        products(2, (0, 1, 2, 3))
+        woven1 = keep.tile([P, 2048], BF16, name="woven1", align_bytes=64)
+        for d, flat in enumerate((woven1[:], arena[:, 496:1520].bitcast(BF16), arena[:, 768:1792].bitcast(BF16))):
+            g[d] = flat.rearrange("p (t q r j) -> p t q r j", t=4, r=2, j=4)
+        weave(on_scalar, 0, 0, 0, 4, 0, 32)
+        weave(on_scalar, 0, 1, 0, 2, 0, 32)
+        weave(on_scalar, 0, 1, 2, 4, 0, 32)
+        quant(0, 0, 2)
+        quant(0, 2, 4)
+        pair_products(0)
+        weave(on_scalar, 1, 0, 1, 4, 0, 32)
+        weave(on_vector, 1, 0, 0, 1, 0, 32)
+        weave(on_scalar, 1, 1, 2, 4, 0, 32)
+        weave(on_vector, 1, 1, 0, 1, 0, 32)
+        weave(on_vector, 1, 1, 1, 2, 0, 32)
+        for t in range(4):
+            quant(1, t, t + 1)
+        pair_products(1)
+        first(0, 0, V)
+        weave(on_scalar, 2, 0, 2, 4, 0, 32)
+        weave(on_vector, 2, 0, 0, 2, 0, 32)
+        first(1, 0, 128)
+        second(0, 0, V)
+        weave(on_scalar, 2, 1, 2, 4, 0, 32)
+        weave(on_vector, 2, 1, 0, 1, 0, 32)
+        weave(on_vector, 2, 1, 1, 2, 0, 32)
+        quant(2, 0, 1)
+        quant(2, 1, 2)
+        quant(2, 2, 4)
+        first(1, 128, V)
+        half_products()
         weave4()
-        quant4()
-        second(1)
+        second(1, 0, 128)
+        second(1, 128, V)
         third(0)
+        quant4()
         third(1)
         last(0)
         last(1)

@@ -28,19 +28,16 @@ def tile_picked_trilin_relu_p_kernel(tc, x_words, x_scales, w1, w2, w3, w4, offs
         nc.vector.memset(scale_table[:].bitcast(I32), 0)
         word_table = keep.tile([P, T], U16, name="word_table", align_bytes=64)
         offsets = keep.tile([P, 48], U16, name="offsets")
+        nc.sync.dma_start(word_table[:].bitcast(I32), x_words[0].bitcast(I32))
         nc.sync.dma_start(offsets[:], offs)
-        nc.scalar.dma_start(word_table[:].bitcast(I32), x_words[0].bitcast(I32))
-        for q in range(4):
-            (nc.sync, nc.scalar)[q % 2].dma_start(scale_table[32 * q : 32 * q + 4, :].bitcast(I32), x_scales[0, 4 * q : 4 * q + 4, :].bitcast(I32))
-        warm_in = keep.tile([P, 1], F32, name="warm_in")
-        warm_out = keep.tile([P, 1], F32, name="warm_out")
-        nc.gpsimd.memset(warm_in[:], 0.0)
-        nc.scalar.activation(warm_out[:], warm_in[:], RELU)
 
         raw = {}
         for name, w, c0, c1 in [("w%d%s" % (d + 1, ("a", "b")[h]), w, 256 * h, 256 * (h + 1)) for d, w in enumerate((w1, w2, w3)) for h in range(2)]:
             raw[name] = keep.tile([P, 4 * (c1 - c0)], F32, name="raw_" + name, tag="raw_" + name, align_bytes=64)[:].rearrange("p (j c) -> p j c", j=4)
             nc.sync.dma_start(raw[name], w.rearrange("(p j) c -> p j c", j=4)[:, :, c0:c1])
+            if name == "w1a":
+                for q in range(4):
+                    nc.sync.dma_start(scale_table[32 * q : 32 * q + 4, :].bitcast(I32), x_scales[0, 4 * q : 4 * q + 4, :].bitcast(I32))
         raw4 = keep.tile([P, 4, N], F32, name="raw4", align_bytes=64)
         for r in range(2):
             nc.sync.dma_start(raw4[r:P:2, :, :], w4.rearrange("(q t r) n -> r q t n", t=4, r=2)[r])
@@ -61,11 +58,10 @@ def tile_picked_trilin_relu_p_kernel(tc, x_words, x_scales, w1, w2, w3, w4, offs
         p12 = keep.tile([P, 2, V, 2], F32, name="p12", align_bytes=64)
         arena = keep.tile([P, 1792], F32, name="arena", align_bytes=64)
         p1 = [arena[:, 512 * u : 512 * (u + 1)].rearrange("p (v e) -> p v e", e=2) for u in range(2)]
-        w4_codes = keep.tile([P, N], U32, name="w4_codes", align_bytes=64)
-        w4_sc = keep.tile([P, N], U8, name="w4_sc", align_bytes=64)
-        z = [keep.tile([P, 128, 4], BF16, name="z%d" % h, align_bytes=64) for h in range(2)]
-        z_codes = [keep.tile([P, 128], U32, name="z_codes%d" % h, align_bytes=64) for h in range(2)]
-        z_sc = [keep.tile([P, 128], U8, name="z_sc%d" % h, align_bytes=64) for h in range(2)]
+        last_in = arena[:, 1024:1792].bitcast(BF16)
+        z = [last_in[:, 512 * (h + 1) : 512 * (h + 2)].rearrange("p (v t) -> p v t", t=4) for h in range(2)]
+        last_codes = keep.tile([P, 3 * 128], U32, name="last_codes", align_bytes=64)
+        last_sc = keep.tile([P, 3 * 128], U8, name="last_sc", align_bytes=64)
         acc = [psum.tile([P, 128], F32, name="acc%d" % h) for h in range(2)]
         res = [keep.tile([P, 128], F32, name="res%d" % h) for h in range(2)]
         g = {}
@@ -110,27 +106,26 @@ def tile_picked_trilin_relu_p_kernel(tc, x_words, x_scales, w1, w2, w3, w4, offs
 
         def third(h):
             nc.vector.tensor_tensor(
-                z[h][:].rearrange("p v (u e) -> p v u e", e=2),
+                z[h].rearrange("p v (u e) -> p v u e", e=2),
                 half_banks[h][:].rearrange("p (u e) v -> p v u e", e=2),
                 p12[:, :, 128 * h : 128 * (h + 1), :].rearrange("p u v e -> p v u e"),
                 MULT,
             )
 
         def weave4():
-            g["w4"] = arena[:, 1024:1280].bitcast(BF16).rearrange("p (n t) -> p n t", t=4)
-            nc.scalar.copy(g["w4"].rearrange("p (c i) t -> p c t i", i=2), raw4[:].rearrange("p t (c i) -> p c t i", i=2))
+            woven4 = last_in[:, 0:512].rearrange("p (n t) -> p n t", t=4)
+            nc.scalar.copy(woven4.rearrange("p (c i) t -> p c t i", i=2), raw4[:].rearrange("p t (c i) -> p c t i", i=2))
 
-        def quant4():
-            nc.vector.quantize_mx(w4_codes[:].bitcast(FP8X4), w4_sc[:], g["w4"].rearrange("p n t -> p (n t)"))
+        def quant_last(c0, c1):
+            nc.vector.quantize_mx(last_codes[:, c0:c1].bitcast(FP8X4), last_sc[:, c0:c1], last_in[:, 4 * c0 : 4 * c1])
 
         def last(h):
-            nc.vector.quantize_mx(z_codes[h][:].bitcast(FP8X4), z_sc[h][:], z[h][:].rearrange("p v t -> p (v t)"))
             nc.tensor.matmul_mx(
                 acc[h][:],
-                lhsT=w4_codes[:].bitcast(FP8X4),
-                lhsT_scale=w4_sc[:],
-                rhs=z_codes[h][:].bitcast(FP8X4),
-                rhs_scale=z_sc[h][:],
+                lhsT=last_codes[:, 0:128].bitcast(FP8X4),
+                lhsT_scale=last_sc[:, 0:128],
+                rhs=last_codes[:, 128 * (h + 1) : 128 * (h + 2)].bitcast(FP8X4),
+                rhs_scale=last_sc[:, 128 * (h + 1) : 128 * (h + 2)],
                 start=True,
                 stop=True,
             )
@@ -160,19 +155,22 @@ def tile_picked_trilin_relu_p_kernel(tc, x_words, x_scales, w1, w2, w3, w4, offs
         weave(on_vector, 2, 0, 0, 2, 0, 32)
         first(1, 0, 128)
         second(0, 0, V)
-        weave(on_scalar, 2, 1, 2, 4, 0, 32)
+        weave(on_scalar, 2, 1, 2, 3, 0, 32)
+        weave(on_scalar, 2, 1, 3, 4, 0, 32)
         weave(on_vector, 2, 1, 0, 1, 0, 32)
         weave(on_vector, 2, 1, 1, 2, 0, 32)
         quant(2, 0, 1)
         quant(2, 1, 2)
-        quant(2, 2, 4)
+        quant(2, 2, 3)
+        quant(2, 3, 4)
         first(1, 128, V)
         half_products()
         weave4()
         second(1, 0, 128)
         second(1, 128, V)
         third(0)
-        quant4()
         third(1)
+        quant_last(0, 256)
         last(0)
+        quant_last(256, 384)
         last(1)

@@ -30,14 +30,14 @@ def tile_picked_trilin_relu_p_kernel(tc, x_words, x_scales, w1, w2, w3, w4, offs
         offsets = keep.tile([P, 48], U16, name="offsets")
         nc.sync.dma_start(word_table[:].bitcast(I32), x_words[0].bitcast(I32))
         nc.sync.dma_start(offsets[:], offs)
-
-        raw = {}
-        for name, w, c0, c1 in [("w%d%s" % (d + 1, ("a", "b")[h]), w, 256 * h, 256 * (h + 1)) for d, w in enumerate((w1, w2, w3)) for h in range(2)]:
-            raw[name] = keep.tile([P, 4 * (c1 - c0)], F32, name="raw_" + name, tag="raw_" + name, align_bytes=64)[:].rearrange("p (j c) -> p j c", j=4)
-            nc.sync.dma_start(raw[name], w.rearrange("(p j) c -> p j c", j=4)[:, :, c0:c1])
-            if name == "w1a":
-                for q in range(4):
-                    nc.sync.dma_start(scale_table[32 * q : 32 * q + 4, :].bitcast(I32), x_scales[0, 4 * q : 4 * q + 4, :].bitcast(I32))
+        raw = [keep.tile([P, 4 * H], F32, name="raw%d" % d, align_bytes=64) for d in range(3)]
+        rows = [w.rearrange("(p j) c -> p (j c)", j=4) for w in (w1, w2, w3)]
+        nc.sync.dma_start(raw[0][:, 0 : 2 * H], rows[0][:, 0 : 2 * H])
+        for q in range(4):
+            nc.sync.dma_start(scale_table[32 * q : 32 * q + 4, :].bitcast(I32), x_scales[0, 4 * q : 4 * q + 4, :].bitcast(I32))
+        nc.sync.dma_start(raw[0][:, 2 * H : 4 * H], rows[0][:, 2 * H : 4 * H])
+        for d in (1, 2):
+            nc.sync.dma_start(raw[d][:], rows[d])
         raw4 = keep.tile([P, 4, N], F32, name="raw4", align_bytes=64)
         for r in range(2):
             nc.sync.dma_start(raw4[r:P:2, :, :], w4.rearrange("(q t r) n -> r q t n", t=4, r=2)[r])
@@ -53,30 +53,33 @@ def tile_picked_trilin_relu_p_kernel(tc, x_words, x_scales, w1, w2, w3, w4, offs
 
         w_codes = [keep.tile([P, H], U32, name="w_codes%d" % d, align_bytes=64) for d in range(3)]
         w_sc = [keep.tile([P, H], U8, name="w_sc%d" % d, align_bytes=64) for d in range(3)]
-        pair_banks = {(d, u): psum.tile([P, 2, V], F32, name="bank%d%d" % (d, u)) for d in range(2) for u in range(2)}
-        half_banks = [psum.tile([P, 4, 128], F32, name="bank2%d" % h) for h in range(2)]
-        p12 = keep.tile([P, 2, V, 2], F32, name="p12", align_bytes=64)
-        arena = keep.tile([P, 1792], F32, name="arena", align_bytes=64)
-        p1 = [arena[:, 512 * u : 512 * (u + 1)].rearrange("p (v e) -> p v e", e=2) for u in range(2)]
-        last_in = arena[:, 1024:1792].bitcast(BF16)
-        z = [last_in[:, 512 * (h + 1) : 512 * (h + 2)].rearrange("p (v t) -> p v t", t=4) for h in range(2)]
+        y1 = [psum.tile([P, 2 * V], F32, name="y1_%d" % u, tag="bank%d" % u) for u in range(2)]
+        y2 = [psum.tile([P, V], F32, name="y2_0"), psum.tile([P, V], F32, name="y2_1"), psum.tile([P, 2 * V], F32, name="y2_23")]
+        y3 = [psum.tile([P, 4, 128], F32, name="y3_%d" % h) for h in range(2)]
+
+        woven01 = keep.tile([P, 4096], BF16, name="woven01", align_bytes=64)[:].rearrange("p (d c) -> p d c", d=2)
+        p1 = woven01[:, 1, :].bitcast(F32)
+        arena = keep.tile([P, 1280], F32, name="arena", align_bytes=64)
+        p12 = arena[:, 0:1024]
+        groups = {(d, t): woven01[:, d, 512 * t : 512 * (t + 1)] for d in range(2) for t in range(4)}
+        groups[2, 0] = p1[:, 0:256].bitcast(BF16)
+        for t, slot in ((1, 1), (2, 2), (3, 4)):
+            groups[2, t] = arena[:, 256 * slot : 256 * (slot + 1)].bitcast(BF16)
+        last_in = keep.tile([P, 1536], BF16, name="last_in", align_bytes=64)
         last_codes = keep.tile([P, 3 * 128], U32, name="last_codes", align_bytes=64)
         last_sc = keep.tile([P, 3 * 128], U8, name="last_sc", align_bytes=64)
-        acc = [psum.tile([P, 128], F32, name="acc%d" % h) for h in range(2)]
         res = [keep.tile([P, 128], F32, name="res%d" % h) for h in range(2)]
-        g = {}
 
-        def weave(copy, d, half, t0, t1, q0, q1):
-            src = raw["w%d%s" % (d + 1, "ab"[half])].rearrange("p j (q t r) -> p t q j r", t=4, r=2)
-            dst = g[d].rearrange("p t q r j -> p t q j r")
-            copy(dst[:, t0:t1, 32 * half + q0 : 32 * half + q1], src[:, t0:t1, q0:q1])
+        def weave(copy, d, t, q0, q1, j0=0, j1=4):
+            src = raw[d][:].rearrange("p (j q t r) -> p t q j r", j=4, t=4, r=2)[:, t, q0:q1, j0:j1]
+            copy(groups[d, t].rearrange("p (q r j) -> p q j r", r=2, j=4)[:, q0:q1, j0:j1], src)
 
-        def quant(d, t0, t1):
-            nc.vector.quantize_mx(
-                w_codes[d][:, 128 * t0 : 128 * t1].bitcast(FP8X4),
-                w_sc[d][:, 128 * t0 : 128 * t1],
-                g[d][:, t0:t1].rearrange("p t q r j -> p (t q r j)"),
-            )
+        def quant(d, t):
+            nc.vector.quantize_mx(w_codes[d][:, 128 * t : 128 * (t + 1)].bitcast(FP8X4), w_sc[d][:, 128 * t : 128 * (t + 1)], groups[d, t])
+
+        def quant_pair(d, u):
+            cols = slice(256 * u, 256 * (u + 1))
+            nc.vector.quantize_mx(w_codes[d][:, cols].bitcast(FP8X4), w_sc[d][:, cols], woven01[:, d, 1024 * u : 1024 * (u + 1)])
 
         def product(bank, d, t, v0, v1):
             nc.tensor.matmul_mx(
@@ -89,39 +92,30 @@ def tile_picked_trilin_relu_p_kernel(tc, x_words, x_scales, w1, w2, w3, w4, offs
                 stop=True,
             )
 
-        def pair_products(d):
-            for t in range(4):
-                product(pair_banks[d, t // 2][:, t % 2, :], d, t, 0, V)
+        def first(t0, t1):
+            nc.scalar.copy(p1[:, V * t0 : V * t1], y1[t0 // 2][:, V * (t0 % 2) : V * (t0 % 2 + t1 - t0)])
 
-        def half_products():
-            for h in range(2):
-                for t in range(4):
-                    product(half_banks[h][:, t, :], 2, t, 128 * h, 128 * (h + 1))
-
-        def first(u, v0, v1):
-            nc.scalar.copy(p1[u][:, v0:v1], pair_banks[0, u][:, :, v0:v1].rearrange("p e v -> p v e"))
-
-        def second(u, v0, v1):
-            nc.vector.tensor_tensor(p12[:, u, v0:v1], pair_banks[1, u][:, :, v0:v1].rearrange("p e v -> p v e"), p1[u][:, v0:v1], MULT)
+        def second(bank, t0, t1):
+            nc.vector.tensor_tensor(p12[:, V * t0 : V * t1], bank, p1[:, V * t0 : V * t1], MULT)
 
         def third(h):
             nc.vector.tensor_tensor(
-                z[h].rearrange("p v (u e) -> p v u e", e=2),
-                half_banks[h][:].rearrange("p (u e) v -> p v u e", e=2),
-                p12[:, :, 128 * h : 128 * (h + 1), :].rearrange("p u v e -> p v u e"),
+                last_in[:, 512 * (h + 1) : 512 * (h + 2)].rearrange("p (c e t) -> p c t e", e=2, t=4),
+                y3[h][:].rearrange("p t (c e) -> p c t e", e=2),
+                p12.rearrange("p (t c e) -> p c t e", t=4, e=2)[:, 64 * h : 64 * (h + 1)],
                 MULT,
             )
 
         def weave4():
-            woven4 = last_in[:, 0:512].rearrange("p (n t) -> p n t", t=4)
-            nc.scalar.copy(woven4.rearrange("p (c i) t -> p c t i", i=2), raw4[:].rearrange("p t (c i) -> p c t i", i=2))
+            nc.scalar.copy(last_in[:, 0:512].rearrange("p (c i t) -> p c t i", i=2, t=4), raw4[:].rearrange("p t (c i) -> p c t i", i=2))
 
         def quant_last(c0, c1):
             nc.vector.quantize_mx(last_codes[:, c0:c1].bitcast(FP8X4), last_sc[:, c0:c1], last_in[:, 4 * c0 : 4 * c1])
 
         def last(h):
+            acc = psum.tile([P, 128], F32, name="acc%d" % h, tag="bank%d" % h)
             nc.tensor.matmul_mx(
-                acc[h][:],
+                acc[:],
                 lhsT=last_codes[:, 0:128].bitcast(FP8X4),
                 lhsT_scale=last_sc[:, 0:128],
                 rhs=last_codes[:, 128 * (h + 1) : 128 * (h + 2)].bitcast(FP8X4),
@@ -129,45 +123,44 @@ def tile_picked_trilin_relu_p_kernel(tc, x_words, x_scales, w1, w2, w3, w4, offs
                 start=True,
                 stop=True,
             )
-            nc.scalar.activation(res[h][:], acc[h][:], RELU)
+            nc.scalar.activation(res[h][:], acc[:], RELU)
             (nc.sync, nc.scalar)[h].dma_start(out[:, 128 * h : 128 * (h + 1)], res[h][:])
 
         on_scalar, on_vector = nc.scalar.copy, nc.vector.tensor_copy
-        woven1 = keep.tile([P, 2048], BF16, name="woven1", align_bytes=64)
-        for d, flat in enumerate((woven1[:], arena[:, 496:1520].bitcast(BF16), arena[:, 768:1792].bitcast(BF16))):
-            g[d] = flat.rearrange("p (t q r j) -> p t q r j", t=4, r=2, j=4)
-        weave(on_scalar, 0, 0, 0, 4, 0, 32)
-        weave(on_scalar, 0, 1, 0, 2, 0, 32)
-        weave(on_scalar, 0, 1, 2, 4, 0, 32)
-        quant(0, 0, 2)
-        quant(0, 2, 4)
-        pair_products(0)
-        weave(on_scalar, 1, 0, 1, 4, 0, 32)
-        weave(on_vector, 1, 0, 0, 1, 0, 32)
-        weave(on_scalar, 1, 1, 2, 4, 0, 32)
-        weave(on_vector, 1, 1, 0, 1, 0, 32)
-        weave(on_vector, 1, 1, 1, 2, 0, 32)
+        for t in range(3):
+            weave(on_scalar, 0, t, 0, 64, 0, 2)
+        for t in range(3):
+            weave(on_scalar, 0, t, 0, 64, 2, 4)
+        weave(on_vector, 0, 3, 0, 64)
+        quant_pair(0, 0)
+        quant(0, 3)
+        quant(0, 2)
+        for t in (0, 1, 3, 2):
+            product(y1[t // 2][:, V * (t % 2) : V * (t % 2 + 1)], 0, t, 0, V)
+        weave(on_scalar, 1, 2, 0, 64)
+        weave(on_scalar, 1, 3, 0, 64)
+        weave(on_vector, 1, 0, 0, 64)
+        weave(on_vector, 1, 1, 0, 64)
         for t in range(4):
-            quant(1, t, t + 1)
-        pair_products(1)
-        first(0, 0, V)
-        weave(on_scalar, 2, 0, 2, 4, 0, 32)
-        weave(on_vector, 2, 0, 0, 2, 0, 32)
-        first(1, 0, 128)
-        second(0, 0, V)
-        weave(on_scalar, 2, 1, 2, 3, 0, 32)
-        weave(on_scalar, 2, 1, 3, 4, 0, 32)
-        weave(on_vector, 2, 1, 0, 1, 0, 32)
-        weave(on_vector, 2, 1, 1, 2, 0, 32)
-        quant(2, 0, 1)
-        quant(2, 1, 2)
-        quant(2, 2, 3)
-        quant(2, 3, 4)
-        first(1, 128, V)
-        half_products()
+            quant(1, t)
+        for t, bank in enumerate((y2[0][:], y2[1][:], y2[2][:, 0:V], y2[2][:, V : 2 * V])):
+            product(bank, 1, t, 0, V)
+        first(0, 1)
+        first(1, 2)
+        first(2, 4)
+        second(y2[0][:], 0, 1)
+        weave(on_scalar, 2, 2, 0, 64)
+        weave(on_scalar, 2, 3, 0, 64)
+        weave(on_vector, 2, 0, 0, 64)
+        weave(on_vector, 2, 1, 0, 64)
+        for t in range(4):
+            quant(2, t)
+        for h in range(2):
+            for t in range(4):
+                product(y3[h][:, t, :], 2, t, 128 * h, 128 * (h + 1))
+        second(y2[1][:], 1, 2)
         weave4()
-        second(1, 0, 128)
-        second(1, 128, V)
+        second(y2[2][:], 2, 4)
         third(0)
         third(1)
         quant_last(0, 256)

@@ -54,16 +54,17 @@ def tile_picked_trilin_relu_p_kernel(tc, x_words, x_scales, w1, w2, w3, w4, offs
         w_codes = [keep.tile([P, H], U32, name="w_codes%d" % d, align_bytes=64) for d in range(3)]
         w_sc = [keep.tile([P, H], U8, name="w_sc%d" % d, align_bytes=64) for d in range(3)]
         y1 = [psum.tile([P, 2 * V], F32, name="y1_%d" % u, tag="bank%d" % u) for u in range(2)]
-        y2 = [psum.tile([P, V], F32, name="y2_0"), psum.tile([P, V], F32, name="y2_1"), psum.tile([P, 2 * V], F32, name="y2_23")]
-        y3 = [psum.tile([P, 4, 128], F32, name="y3_%d" % h) for h in range(2)]
+        y2 = [psum.tile([P, V], F32, name="y2_0", tag="single0"), psum.tile([P, V], F32, name="y2_1", tag="single1"), psum.tile([P, 2 * V], F32, name="y2_23")]
+        y2_of = [y2[0][:], y2[1][:], y2[2][:, 0:V], y2[2][:, V : 2 * V]]
+        y3 = []
 
         woven01 = keep.tile([P, 4096], BF16, name="woven01", align_bytes=64)[:].rearrange("p (d c) -> p d c", d=2)
         p1 = woven01[:, 1, :].bitcast(F32)
-        arena = keep.tile([P, 1280], F32, name="arena", align_bytes=64)
+        arena = keep.tile([P, 1536], F32, name="arena", align_bytes=64)
         p12 = arena[:, 0:1024]
         groups = {(d, t): woven01[:, d, 512 * t : 512 * (t + 1)] for d in range(2) for t in range(4)}
         groups[2, 0] = p1[:, 0:256].bitcast(BF16)
-        for t, slot in ((1, 1), (2, 2), (3, 4)):
+        for t, slot in ((1, 4), (2, 2), (3, 5)):
             groups[2, t] = arena[:, 256 * slot : 256 * (slot + 1)].bitcast(BF16)
         last_in = keep.tile([P, 1536], BF16, name="last_in", align_bytes=64)
         last_codes = keep.tile([P, 3 * 128], U32, name="last_codes", align_bytes=64)
@@ -77,10 +78,6 @@ def tile_picked_trilin_relu_p_kernel(tc, x_words, x_scales, w1, w2, w3, w4, offs
         def quant(d, t):
             nc.vector.quantize_mx(w_codes[d][:, 128 * t : 128 * (t + 1)].bitcast(FP8X4), w_sc[d][:, 128 * t : 128 * (t + 1)], groups[d, t])
 
-        def quant_pair(d, u):
-            cols = slice(256 * u, 256 * (u + 1))
-            nc.vector.quantize_mx(w_codes[d][:, cols].bitcast(FP8X4), w_sc[d][:, cols], woven01[:, d, 1024 * u : 1024 * (u + 1)])
-
         def product(bank, d, t, v0, v1):
             nc.tensor.matmul_mx(
                 bank,
@@ -92,11 +89,11 @@ def tile_picked_trilin_relu_p_kernel(tc, x_words, x_scales, w1, w2, w3, w4, offs
                 stop=True,
             )
 
-        def first(t0, t1):
-            nc.scalar.copy(p1[:, V * t0 : V * t1], y1[t0 // 2][:, V * (t0 % 2) : V * (t0 % 2 + t1 - t0)])
+        def first(t):
+            nc.scalar.copy(p1[:, V * (t % 3) : V * (t % 3 + 1)], y1[t // 2][:, V * (t % 2) : V * (t % 2 + 1)])
 
-        def second(bank, t0, t1):
-            nc.vector.tensor_tensor(p12[:, V * t0 : V * t1], bank, p1[:, V * t0 : V * t1], MULT)
+        def second(t):
+            nc.vector.tensor_tensor(p12[:, V * t : V * (t + 1)], y2_of[t], p1[:, V * (t % 3) : V * (t % 3 + 1)], MULT)
 
         def third(h):
             nc.vector.tensor_tensor(
@@ -113,7 +110,7 @@ def tile_picked_trilin_relu_p_kernel(tc, x_words, x_scales, w1, w2, w3, w4, offs
             nc.vector.quantize_mx(last_codes[:, c0:c1].bitcast(FP8X4), last_sc[:, c0:c1], last_in[:, 4 * c0 : 4 * c1])
 
         def last(h):
-            acc = psum.tile([P, 128], F32, name="acc%d" % h, tag="bank%d" % h)
+            acc = psum.tile([P, 128], F32, name="acc%d" % h, tag="single%d" % h)
             nc.tensor.matmul_mx(
                 acc[:],
                 lhsT=last_codes[:, 0:128].bitcast(FP8X4),
@@ -131,11 +128,12 @@ def tile_picked_trilin_relu_p_kernel(tc, x_words, x_scales, w1, w2, w3, w4, offs
             weave(on_scalar, 0, t, 0, 64, 0, 2)
         for t in range(3):
             weave(on_scalar, 0, t, 0, 64, 2, 4)
+        quant(0, 0)
+        quant(0, 1)
         weave(on_vector, 0, 3, 0, 64)
-        quant_pair(0, 0)
-        quant(0, 3)
         quant(0, 2)
-        for t in (0, 1, 3, 2):
+        quant(0, 3)
+        for t in range(4):
             product(y1[t // 2][:, V * (t % 2) : V * (t % 2 + 1)], 0, t, 0, V)
         weave(on_scalar, 1, 2, 0, 64)
         weave(on_scalar, 1, 3, 0, 64)
@@ -143,24 +141,27 @@ def tile_picked_trilin_relu_p_kernel(tc, x_words, x_scales, w1, w2, w3, w4, offs
         weave(on_vector, 1, 1, 0, 64)
         for t in range(4):
             quant(1, t)
-        for t, bank in enumerate((y2[0][:], y2[1][:], y2[2][:, 0:V], y2[2][:, V : 2 * V])):
-            product(bank, 1, t, 0, V)
-        first(0, 1)
-        first(1, 2)
-        first(2, 4)
-        second(y2[0][:], 0, 1)
-        weave(on_scalar, 2, 2, 0, 64)
+        for t in range(4):
+            product(y2_of[t], 1, t, 0, V)
+        for t in range(3):
+            first(t)
+        second(0)
+        second(1)
+        weave(on_scalar, 2, 2, 16, 64)
         weave(on_scalar, 2, 3, 0, 64)
         weave(on_vector, 2, 0, 0, 64)
         weave(on_vector, 2, 1, 0, 64)
+        weave(on_vector, 2, 2, 0, 16)
         for t in range(4):
             quant(2, t)
+        first(3)
         for h in range(2):
+            y3.append(psum.tile([P, 4, 128], F32, name="y3_%d" % h, tag="bank%d" % h))
             for t in range(4):
                 product(y3[h][:, t, :], 2, t, 128 * h, 128 * (h + 1))
-        second(y2[1][:], 1, 2)
         weave4()
-        second(y2[2][:], 2, 4)
+        second(2)
+        second(3)
         third(0)
         third(1)
         quant_last(0, 256)

@@ -14,6 +14,7 @@ U8 = mybir.dt.uint8
 FP8X4 = mybir.dt.float8_e4m3fn_x4
 FP4X4 = mybir.dt.float4_e2m1fn_x4
 MULT = mybir.AluOpType.mult
+ADD = mybir.AluOpType.add
 RELU = mybir.ActivationFunctionType.Relu
 P = 128
 
@@ -75,6 +76,10 @@ def tile_picked_trilin_relu_p_kernel(tc, x_words, x_scales, w1, w2, w3, w4, offs
             src = raw[d][:].rearrange("p (j q t r) -> p t q j r", j=4, t=4, r=2)[:, t, q0:q1, j0:j1]
             copy(groups[d, t].rearrange("p (q r j) -> p q j r", r=2, j=4)[:, q0:q1, j0:j1], src)
 
+        def weave_on_gpsimd(d, t):
+            src = raw[d][:].rearrange("p (j q t r) -> p t q r j", j=4, t=4, r=2)[:, t]
+            nc.gpsimd.tensor_scalar(groups[d, t].rearrange("p (q r j) -> p q r j", r=2, j=4), src, 1.0, 0.0, MULT, ADD)
+
         def quant(d, t):
             nc.vector.quantize_mx(w_codes[d][:, 128 * t : 128 * (t + 1)].bitcast(FP8X4), w_sc[d][:, 128 * t : 128 * (t + 1)], groups[d, t])
 
@@ -130,7 +135,7 @@ def tile_picked_trilin_relu_p_kernel(tc, x_words, x_scales, w1, w2, w3, w4, offs
             weave(on_scalar, 0, t, 0, 64, 2, 4)
         quant(0, 0)
         quant(0, 1)
-        weave(on_vector, 0, 3, 0, 64)
+        weave_on_gpsimd(0, 3)
         quant(0, 2)
         quant(0, 3)
         for t in range(4):

@@ -17,6 +17,7 @@ MULT = mybir.AluOpType.mult
 ADD = mybir.AluOpType.add
 RELU = mybir.ActivationFunctionType.Relu
 P = 128
+CUT = 3 * H + H // 2
 
 
 def tile_picked_trilin_relu_p_kernel(tc, x_words, x_scales, w1, w2, w3, w4, offs, out):
@@ -38,7 +39,8 @@ def tile_picked_trilin_relu_p_kernel(tc, x_words, x_scales, w1, w2, w3, w4, offs
             nc.sync.dma_start(scale_table[32 * q : 32 * q + 4, :].bitcast(I32), x_scales[0, 4 * q : 4 * q + 4, :].bitcast(I32))
         nc.sync.dma_start(raw[0][:, 2 * H : 4 * H], rows[0][:, 2 * H : 4 * H])
         for d in (1, 2):
-            nc.sync.dma_start(raw[d][:], rows[d])
+            for c0, c1 in ((0, CUT), (CUT, 4 * H)):
+                nc.sync.dma_start(raw[d][:, c0:c1], rows[d][:, c0:c1])
         raw4 = keep.tile([P, 4, N], F32, name="raw4", align_bytes=64)
         for r in range(2):
             nc.sync.dma_start(raw4[r:P:2, :, :], w4.rearrange("(q t r) n -> r q t n", t=4, r=2)[r])
@@ -59,13 +61,15 @@ def tile_picked_trilin_relu_p_kernel(tc, x_words, x_scales, w1, w2, w3, w4, offs
         y2_of = [y2[0][:], y2[1][:], y2[2][:, 0:V], y2[2][:, V : 2 * V]]
         y3 = []
 
-        woven01 = keep.tile([P, 4096], BF16, name="woven01", align_bytes=64)[:].rearrange("p (d c) -> p d c", d=2)
+        flat01 = keep.tile([P, 4096], BF16, name="flat01", align_bytes=64)
+        woven01 = flat01[:].rearrange("p (d c) -> p d c", d=2)
         p1 = woven01[:, 1, :].bitcast(F32)
-        arena = keep.tile([P, 1536], F32, name="arena", align_bytes=64)
+        arena = keep.tile([P, 1280], F32, name="arena", align_bytes=64)
         p12 = arena[:, 0:1024]
         groups = {(d, t): woven01[:, d, 512 * t : 512 * (t + 1)] for d in range(2) for t in range(4)}
-        groups[2, 0] = p1[:, 0:256].bitcast(BF16)
-        for t, slot in ((1, 4), (2, 2), (3, 5)):
+        groups[2, 0] = woven01[:, 0, 1536:2048]
+        groups[2, 1] = woven01[:, 1, 0:512]
+        for t, slot in ((2, 2), (3, 4)):
             groups[2, t] = arena[:, 256 * slot : 256 * (slot + 1)].bitcast(BF16)
         last_in = keep.tile([P, 1536], BF16, name="last_in", align_bytes=64)
         last_codes = keep.tile([P, 3 * 128], U32, name="last_codes", align_bytes=64)
@@ -75,6 +79,10 @@ def tile_picked_trilin_relu_p_kernel(tc, x_words, x_scales, w1, w2, w3, w4, offs
         def weave(copy, d, t, q0, q1, j0=0, j1=4):
             src = raw[d][:].rearrange("p (j q t r) -> p t q j r", j=4, t=4, r=2)[:, t, q0:q1, j0:j1]
             copy(groups[d, t].rearrange("p (q r j) -> p q j r", r=2, j=4)[:, q0:q1, j0:j1], src)
+
+        def weave_pair(copy, d, t0, start, q0, q1):
+            src = raw[d][:].rearrange("p (j q t r) -> p t q j r", j=4, t=4, r=2)[:, t0 : t0 + 2, q0:q1]
+            copy(flat01[:, start : start + 1024].rearrange("p (t q r j) -> p t q j r", t=2, r=2, j=4)[:, :, q0:q1], src)
 
         def weave_on_gpsimd(d, t):
             src = raw[d][:].rearrange("p (j q t r) -> p t q r j", j=4, t=4, r=2)[:, t]
@@ -140,10 +148,12 @@ def tile_picked_trilin_relu_p_kernel(tc, x_words, x_scales, w1, w2, w3, w4, offs
         quant(0, 3)
         for t in range(4):
             product(y1[t // 2][:, V * (t % 2) : V * (t % 2 + 1)], 0, t, 0, V)
-        weave(on_scalar, 1, 2, 0, 64)
-        weave(on_scalar, 1, 3, 0, 64)
-        weave(on_vector, 1, 0, 0, 64)
-        weave(on_vector, 1, 1, 0, 64)
+        weave_pair(on_scalar, 1, 2, 3072, 0, 32)
+        weave(on_scalar, 1, 2, 32, 64)
+        weave(on_scalar, 1, 3, 32, 64)
+        weave_pair(on_vector, 1, 0, 2048, 0, 32)
+        weave(on_vector, 1, 0, 32, 64)
+        weave(on_vector, 1, 1, 32, 64)
         for t in range(4):
             quant(1, t)
         for t in range(4):
@@ -152,10 +162,13 @@ def tile_picked_trilin_relu_p_kernel(tc, x_words, x_scales, w1, w2, w3, w4, offs
             first(t)
         second(0)
         second(1)
-        weave(on_scalar, 2, 2, 16, 64)
-        weave(on_scalar, 2, 3, 0, 64)
-        weave(on_vector, 2, 0, 0, 64)
-        weave(on_vector, 2, 1, 0, 64)
+        weave(on_scalar, 2, 2, 16, 32)
+        weave(on_scalar, 2, 3, 0, 32)
+        weave(on_scalar, 2, 2, 32, 64)
+        weave(on_scalar, 2, 3, 32, 64)
+        weave_pair(on_vector, 2, 0, 1536, 0, 32)
+        weave(on_vector, 2, 0, 32, 64)
+        weave(on_vector, 2, 1, 32, 64)
         weave(on_vector, 2, 2, 0, 16)
         for t in range(4):
             quant(2, t)

@@ -14,7 +14,6 @@ U8 = mybir.dt.uint8
 FP8X4 = mybir.dt.float8_e4m3fn_x4
 FP4X4 = mybir.dt.float4_e2m1fn_x4
 MULT = mybir.AluOpType.mult
-ADD = mybir.AluOpType.add
 RELU = mybir.ActivationFunctionType.Relu
 P = 128
 CUT = 3 * H + H // 2
@@ -56,21 +55,25 @@ def tile_picked_trilin_relu_p_kernel(tc, x_words, x_scales, w1, w2, w3, w4, offs
 
         w_codes = [keep.tile([P, H], U32, name="w_codes%d" % d, align_bytes=64) for d in range(3)]
         w_sc = [keep.tile([P, H], U8, name="w_sc%d" % d, align_bytes=64) for d in range(3)]
-        y1 = [psum.tile([P, 2 * V], F32, name="y1_%d" % u, tag="bank%d" % u) for u in range(2)]
+        y1 = [psum.tile([P, 2 * V], F32, name="y1_01", tag="bank0"), psum.tile([P, V], F32, name="y1_2"), psum.tile([P, V], F32, name="y1_3", tag="bank1")]
+        y1_of = [y1[0][:, 0:V], y1[0][:, V : 2 * V], y1[1][:], y1[2][:]]
         y2 = [psum.tile([P, V], F32, name="y2_0", tag="single0"), psum.tile([P, V], F32, name="y2_1", tag="single1"), psum.tile([P, 2 * V], F32, name="y2_23")]
         y2_of = [y2[0][:], y2[1][:], y2[2][:, 0:V], y2[2][:, V : 2 * V]]
         y3 = []
 
-        flat01 = keep.tile([P, 4096], BF16, name="flat01", align_bytes=64)
-        woven01 = flat01[:].rearrange("p (d c) -> p d c", d=2)
-        p1 = woven01[:, 1, :].bitcast(F32)
+        woven1 = keep.tile([P, 2048], BF16, name="woven1", align_bytes=64)
+        lower2 = keep.tile([P, 1024], BF16, name="lower2", tag="lower2", align_bytes=64)
+        upper2 = keep.tile([P, 1024], BF16, name="upper2", align_bytes=64)
         arena = keep.tile([P, 1280], F32, name="arena", align_bytes=64)
         p12 = arena[:, 0:1024]
-        groups = {(d, t): woven01[:, d, 512 * t : 512 * (t + 1)] for d in range(2) for t in range(4)}
-        groups[2, 0] = woven01[:, 0, 1536:2048]
-        groups[2, 1] = woven01[:, 1, 0:512]
-        for t, slot in ((2, 2), (3, 4)):
-            groups[2, t] = arena[:, 256 * slot : 256 * (slot + 1)].bitcast(BF16)
+        lower = {1: lower2[:], 2: raw[1][:, 0:512].bitcast(BF16)}
+        groups = {(0, t): woven1[:, 512 * t : 512 * (t + 1)] for t in range(4)}
+        for t in range(4):
+            groups[1, t] = (lower2, upper2)[t // 2][:, 512 * (t % 2) : 512 * (t % 2 + 1)]
+        codes = {(d, t): w_codes[d][:, 128 * t : 128 * (t + 1)] for d in range(3) for t in range(4)}
+        groups[2, 0], groups[2, 1] = lower[2][:, 0:512], lower[2][:, 512:1024]
+        groups[2, 2], groups[2, 3] = arena[:, 512:768].bitcast(BF16), arena[:, 1024:1280].bitcast(BF16)
+        p1_of = [raw[1][:, H * (t % 3) : H * (t % 3) + V] for t in range(4)]
         last_in = keep.tile([P, 1536], BF16, name="last_in", align_bytes=64)
         last_codes = keep.tile([P, 3 * 128], U32, name="last_codes", align_bytes=64)
         last_sc = keep.tile([P, 3 * 128], U8, name="last_sc", align_bytes=64)
@@ -80,21 +83,21 @@ def tile_picked_trilin_relu_p_kernel(tc, x_words, x_scales, w1, w2, w3, w4, offs
             src = raw[d][:].rearrange("p (j q t r) -> p t q j r", j=4, t=4, r=2)[:, t, q0:q1, j0:j1]
             copy(groups[d, t].rearrange("p (q r j) -> p q j r", r=2, j=4)[:, q0:q1, j0:j1], src)
 
-        def weave_pair(copy, d, t0, start, q0, q1):
-            src = raw[d][:].rearrange("p (j q t r) -> p t q j r", j=4, t=4, r=2)[:, t0 : t0 + 2, q0:q1]
-            copy(flat01[:, start : start + 1024].rearrange("p (t q r j) -> p t q j r", t=2, r=2, j=4)[:, :, q0:q1], src)
+        def weave_lower(d, q0, q1):
+            src = raw[d][:].rearrange("p (j q t r) -> p t q j r", j=4, t=4, r=2)[:, 0:2, q0:q1]
+            nc.vector.tensor_copy(lower[d].rearrange("p (t q r j) -> p t q j r", t=2, r=2, j=4)[:, :, q0:q1], src)
 
-        def weave_on_gpsimd(d, t):
-            src = raw[d][:].rearrange("p (j q t r) -> p t q r j", j=4, t=4, r=2)[:, t]
-            nc.gpsimd.tensor_scalar(groups[d, t].rearrange("p (q r j) -> p q r j", r=2, j=4), src, 1.0, 0.0, MULT, ADD)
+        def weave_first_rows():
+            src = raw[0][:].rearrange("p (j q t r) -> p t q j r", j=4, t=4, r=2)[:, 0:3, :, 0:2]
+            nc.scalar.copy(woven1[:].rearrange("p (t q r j) -> p t q j r", t=4, r=2, j=4)[:, 0:3, :, 0:2], src)
 
         def quant(d, t):
-            nc.vector.quantize_mx(w_codes[d][:, 128 * t : 128 * (t + 1)].bitcast(FP8X4), w_sc[d][:, 128 * t : 128 * (t + 1)], groups[d, t])
+            nc.vector.quantize_mx(codes[d, t].bitcast(FP8X4), w_sc[d][:, 128 * t : 128 * (t + 1)], groups[d, t])
 
         def product(bank, d, t, v0, v1):
             nc.tensor.matmul_mx(
                 bank,
-                lhsT=w_codes[d][:, 128 * t : 128 * (t + 1)].bitcast(FP8X4),
+                lhsT=codes[d, t].bitcast(FP8X4),
                 lhsT_scale=w_sc[d][:, 128 * t : 128 * (t + 1)],
                 rhs=x_codes[d][:, v0:v1].bitcast(FP4X4),
                 rhs_scale=x_sc[d][:, v0:v1],
@@ -103,10 +106,10 @@ def tile_picked_trilin_relu_p_kernel(tc, x_words, x_scales, w1, w2, w3, w4, offs
             )
 
         def first(t):
-            nc.scalar.copy(p1[:, V * (t % 3) : V * (t % 3 + 1)], y1[t // 2][:, V * (t % 2) : V * (t % 2 + 1)])
+            nc.scalar.copy(p1_of[t], y1_of[t])
 
         def second(t):
-            nc.vector.tensor_tensor(p12[:, V * t : V * (t + 1)], y2_of[t], p1[:, V * (t % 3) : V * (t % 3 + 1)], MULT)
+            nc.vector.tensor_tensor(p12[:, V * t : V * (t + 1)], y2_of[t], p1_of[t], MULT)
 
         def third(h):
             nc.vector.tensor_tensor(
@@ -137,27 +140,30 @@ def tile_picked_trilin_relu_p_kernel(tc, x_words, x_scales, w1, w2, w3, w4, offs
             (nc.sync, nc.scalar)[h].dma_start(out[:, 128 * h : 128 * (h + 1)], res[h][:])
 
         on_scalar, on_vector = nc.scalar.copy, nc.vector.tensor_copy
-        for t in range(3):
-            weave(on_scalar, 0, t, 0, 64, 0, 2)
+        weave_first_rows()
         for t in range(3):
             weave(on_scalar, 0, t, 0, 64, 2, 4)
         quant(0, 0)
         quant(0, 1)
-        weave_on_gpsimd(0, 3)
+        weave(on_scalar, 0, 3, 0, 64)
         quant(0, 2)
-        quant(0, 3)
-        for t in range(4):
-            product(y1[t // 2][:, V * (t % 2) : V * (t % 2 + 1)], 0, t, 0, V)
-        weave_pair(on_scalar, 1, 2, 3072, 0, 32)
+        for t in range(3):
+            product(y1_of[t], 0, t, 0, V)
+        weave(on_scalar, 1, 2, 16, 32)
+        weave(on_scalar, 1, 3, 0, 32)
         weave(on_scalar, 1, 2, 32, 64)
         weave(on_scalar, 1, 3, 32, 64)
-        weave_pair(on_vector, 1, 0, 2048, 0, 32)
+        weave_lower(1, 0, 32)
         weave(on_vector, 1, 0, 32, 64)
         weave(on_vector, 1, 1, 32, 64)
+        weave(on_vector, 1, 2, 0, 16)
         for t in range(4):
             quant(1, t)
         for t in range(4):
             product(y2_of[t], 1, t, 0, V)
+        codes[0, 3] = keep.tile([P, 128], U32, name="codes_late", tag="lower2", align_bytes=64)[:]
+        quant(0, 3)
+        product(y1_of[3], 0, 3, 0, V)
         for t in range(3):
             first(t)
         second(0)
@@ -166,7 +172,7 @@ def tile_picked_trilin_relu_p_kernel(tc, x_words, x_scales, w1, w2, w3, w4, offs
         weave(on_scalar, 2, 3, 0, 32)
         weave(on_scalar, 2, 2, 32, 64)
         weave(on_scalar, 2, 3, 32, 64)
-        weave_pair(on_vector, 2, 0, 1536, 0, 32)
+        weave_lower(2, 0, 32)
         weave(on_vector, 2, 0, 32, 64)
         weave(on_vector, 2, 1, 32, 64)
         weave(on_vector, 2, 2, 0, 16)

@@ -137,7 +137,6 @@ def tile_picked_trilin_relu_p_kernel(tc, x_words, x_scales, w1, w2, w3, w4, offs
                 stop=True,
             )
             nc.scalar.activation(res[h][:], acc[:], RELU)
-            (nc.sync, nc.scalar)[h].dma_start(out[:, 128 * h : 128 * (h + 1)], res[h][:])
 
         on_scalar, on_vector = nc.scalar.copy, nc.vector.tensor_copy
         weave_first_rows()
@@ -192,3 +191,5 @@ def tile_picked_trilin_relu_p_kernel(tc, x_words, x_scales, w1, w2, w3, w4, offs
         last(0)
         quant_last(256, 384)
         last(1)
+        for h in range(2):
+            nc.scalar.dma_start(out[:, 128 * h : 128 * (h + 1)], res[h][:])

@@ -15,8 +15,14 @@ FP8X4 = mybir.dt.float8_e4m3fn_x4
 FP4X4 = mybir.dt.float4_e2m1fn_x4
 MULT = mybir.AluOpType.mult
 RELU = mybir.ActivationFunctionType.Relu
+
 P = 128
+GROUP = 4 * P
+HALF = V // 2
+Q = H // 8
+LIST_COLS = V // 16
 CUT = 3 * H + H // 2
+Q_VECTOR = 16
 
 
 def tile_picked_trilin_relu_p_kernel(tc, x_words, x_scales, w1, w2, w3, w4, offs, out):
@@ -28,14 +34,17 @@ def tile_picked_trilin_relu_p_kernel(tc, x_words, x_scales, w1, w2, w3, w4, offs
         scale_table = keep.tile([P, T], U8, name="scale_table", align_bytes=64)
         nc.vector.memset(scale_table[:].bitcast(I32), 0)
         word_table = keep.tile([P, T], U16, name="word_table", align_bytes=64)
-        offsets = keep.tile([P, 48], U16, name="offsets")
+        offsets = keep.tile([P, 3 * LIST_COLS], U16, name="offsets")
         nc.sync.dma_start(word_table[:].bitcast(I32), x_words[0].bitcast(I32))
         nc.sync.dma_start(offsets[:], offs)
         raw = [keep.tile([P, 4 * H], F32, name="raw%d" % d, align_bytes=64) for d in range(3)]
         rows = [w.rearrange("(p j) c -> p (j c)", j=4) for w in (w1, w2, w3)]
         nc.sync.dma_start(raw[0][:, 0 : 2 * H], rows[0][:, 0 : 2 * H])
-        for q in range(4):
-            nc.sync.dma_start(scale_table[32 * q : 32 * q + 4, :].bitcast(I32), x_scales[0, 4 * q : 4 * q + 4, :].bitcast(I32))
+        for quadrant in range(4):
+            nc.sync.dma_start(
+                scale_table[32 * quadrant : 32 * quadrant + 4, :].bitcast(I32),
+                x_scales[0, 4 * quadrant : 4 * quadrant + 4, :].bitcast(I32),
+            )
         nc.sync.dma_start(raw[0][:, 2 * H : 4 * H], rows[0][:, 2 * H : 4 * H])
         for d in (1, 2):
             for c0, c1 in ((0, CUT), (CUT, 4 * H)):
@@ -47,149 +56,148 @@ def tile_picked_trilin_relu_p_kernel(tc, x_words, x_scales, w1, w2, w3, w4, offs
         words01 = keep.tile([P, 2 * V], U16, name="words01", align_bytes=64)
         words2 = keep.tile([P, V], U16, name="words2", align_bytes=64)
         picked_scales = keep.tile([P, 3 * V], U8, name="picked_scales", align_bytes=64)
-        nc.vector.tensor_copy(words01[:], word_table[:].indirect(offsets[:, 0:32]))
-        nc.vector.tensor_copy(words2[:], word_table[:].indirect(offsets[:, 32:48]))
+        nc.vector.tensor_copy(words01[:], word_table[:].indirect(offsets[:, 0 : 2 * LIST_COLS]))
+        nc.vector.tensor_copy(words2[:], word_table[:].indirect(offsets[:, 2 * LIST_COLS : 3 * LIST_COLS]))
         nc.vector.tensor_copy(picked_scales[:], scale_table[:].indirect(offsets[:]))
         x_codes = [words01[:, 0:V], words01[:, V : 2 * V], words2[:]]
         x_sc = [picked_scales[:, V * d : V * (d + 1)] for d in range(3)]
 
         w_codes = [keep.tile([P, H], U32, name="w_codes%d" % d, align_bytes=64) for d in range(3)]
         w_sc = [keep.tile([P, H], U8, name="w_sc%d" % d, align_bytes=64) for d in range(3)]
-        y1 = [psum.tile([P, 2 * V], F32, name="y1_01", tag="bank0"), psum.tile([P, V], F32, name="y1_2"), psum.tile([P, V], F32, name="y1_3", tag="bank1")]
-        y1_of = [y1[0][:, 0:V], y1[0][:, V : 2 * V], y1[1][:], y1[2][:]]
-        y2 = [psum.tile([P, V], F32, name="y2_0", tag="single0"), psum.tile([P, V], F32, name="y2_1", tag="single1"), psum.tile([P, 2 * V], F32, name="y2_23")]
-        y2_of = [y2[0][:], y2[1][:], y2[2][:, 0:V], y2[2][:, V : 2 * V]]
+
+        y1_01 = psum.tile([P, 2 * V], F32, name="y1_01", tag="bank0")
+        y1_2 = psum.tile([P, V], F32, name="y1_2")
+        y1_3 = psum.tile([P, V], F32, name="y1_3", tag="bank1")
+        y1 = [y1_01[:, 0:V], y1_01[:, V : 2 * V], y1_2[:], y1_3[:]]
+        y2_0 = psum.tile([P, V], F32, name="y2_0", tag="single0")
+        y2_1 = psum.tile([P, V], F32, name="y2_1", tag="single1")
+        y2_23 = psum.tile([P, 2 * V], F32, name="y2_23")
+        y2 = [y2_0[:], y2_1[:], y2_23[:, 0:V], y2_23[:, V : 2 * V]]
         y3 = []
 
-        woven1 = keep.tile([P, 2048], BF16, name="woven1", align_bytes=64)
-        lower2 = keep.tile([P, 1024], BF16, name="lower2", tag="lower2", align_bytes=64)
-        upper2 = keep.tile([P, 1024], BF16, name="upper2", align_bytes=64)
-        arena = keep.tile([P, 1280], F32, name="arena", align_bytes=64)
-        p12 = arena[:, 0:1024]
-        lower = {1: lower2[:], 2: raw[1][:, 0:512].bitcast(BF16)}
-        groups = {(0, t): woven1[:, 512 * t : 512 * (t + 1)] for t in range(4)}
+        woven1 = keep.tile([P, 4 * GROUP], BF16, name="woven1", align_bytes=64)
+        lower2 = keep.tile([P, 2 * GROUP], BF16, name="lower2", tag="lower2", align_bytes=64)
+        upper2 = keep.tile([P, 2 * GROUP], BF16, name="upper2", align_bytes=64)
+        arena = keep.tile([P, 5 * V], F32, name="arena", align_bytes=64)
+        y12 = arena[:, 0 : 4 * V]
+        y1_sbuf = [raw[1][:, H * (t % 3) : H * (t % 3) + V] for t in range(4)]
+        lower = {1: lower2[:], 2: raw[1][:, 0:H].bitcast(BF16)}
+        groups = {(0, t): woven1[:, GROUP * t : GROUP * (t + 1)] for t in range(4)}
         for t in range(4):
-            groups[1, t] = (lower2, upper2)[t // 2][:, 512 * (t % 2) : 512 * (t % 2 + 1)]
-        codes = {(d, t): w_codes[d][:, 128 * t : 128 * (t + 1)] for d in range(3) for t in range(4)}
-        groups[2, 0], groups[2, 1] = lower[2][:, 0:512], lower[2][:, 512:1024]
-        groups[2, 2], groups[2, 3] = arena[:, 512:768].bitcast(BF16), arena[:, 1024:1280].bitcast(BF16)
-        p1_of = [raw[1][:, H * (t % 3) : H * (t % 3) + V] for t in range(4)]
-        last_in = keep.tile([P, 1536], BF16, name="last_in", align_bytes=64)
-        last_codes = keep.tile([P, 3 * 128], U32, name="last_codes", align_bytes=64)
-        last_sc = keep.tile([P, 3 * 128], U8, name="last_sc", align_bytes=64)
-        res = [keep.tile([P, 128], F32, name="res%d" % h) for h in range(2)]
+            groups[1, t] = (lower2, upper2)[t // 2][:, GROUP * (t % 2) : GROUP * (t % 2 + 1)]
+        groups[2, 0], groups[2, 1] = lower[2][:, 0:GROUP], lower[2][:, GROUP : 2 * GROUP]
+        groups[2, 2], groups[2, 3] = arena[:, 2 * V : 3 * V].bitcast(BF16), arena[:, 4 * V : 5 * V].bitcast(BF16)
+        codes = {(d, t): w_codes[d][:, P * t : P * (t + 1)] for d in range(3) for t in range(4)}
+
+        last_in = keep.tile([P, 4 * (N + V)], BF16, name="last_in", align_bytes=64)
+        last_codes = keep.tile([P, N + V], U32, name="last_codes", align_bytes=64)
+        last_sc = keep.tile([P, N + V], U8, name="last_sc", align_bytes=64)
+        res = keep.tile([P, V], F32, name="res")
+
+        on_scalar, on_vector = nc.scalar.copy, nc.vector.tensor_copy
 
         def weave(copy, d, t, q0, q1, j0=0, j1=4):
             src = raw[d][:].rearrange("p (j q t r) -> p t q j r", j=4, t=4, r=2)[:, t, q0:q1, j0:j1]
             copy(groups[d, t].rearrange("p (q r j) -> p q j r", r=2, j=4)[:, q0:q1, j0:j1], src)
 
-        def weave_lower(d, q0, q1):
-            src = raw[d][:].rearrange("p (j q t r) -> p t q j r", j=4, t=4, r=2)[:, 0:2, q0:q1]
-            nc.vector.tensor_copy(lower[d].rearrange("p (t q r j) -> p t q j r", t=2, r=2, j=4)[:, :, q0:q1], src)
+        def weave_shared(d):
+            weave(on_scalar, d, 2, Q_VECTOR, Q // 2)
+            weave(on_scalar, d, 3, 0, Q // 2)
+            weave(on_scalar, d, 2, Q // 2, Q)
+            weave(on_scalar, d, 3, Q // 2, Q)
+            src = raw[d][:].rearrange("p (j q t r) -> p t q j r", j=4, t=4, r=2)[:, 0:2, 0 : Q // 2]
+            on_vector(lower[d].rearrange("p (t q r j) -> p t q j r", t=2, r=2, j=4)[:, :, 0 : Q // 2], src)
+            weave(on_vector, d, 0, Q // 2, Q)
+            weave(on_vector, d, 1, Q // 2, Q)
+            weave(on_vector, d, 2, 0, Q_VECTOR)
 
-        def weave_first_rows():
-            src = raw[0][:].rearrange("p (j q t r) -> p t q j r", j=4, t=4, r=2)[:, 0:3, :, 0:2]
-            nc.scalar.copy(woven1[:].rearrange("p (t q r j) -> p t q j r", t=4, r=2, j=4)[:, 0:3, :, 0:2], src)
-
-        def quant(d, t):
-            nc.vector.quantize_mx(codes[d, t].bitcast(FP8X4), w_sc[d][:, 128 * t : 128 * (t + 1)], groups[d, t])
+        def quantise(d, t):
+            nc.vector.quantize_mx(codes[d, t].bitcast(FP8X4), w_sc[d][:, P * t : P * (t + 1)], groups[d, t])
 
         def product(bank, d, t, v0, v1):
             nc.tensor.matmul_mx(
                 bank,
                 lhsT=codes[d, t].bitcast(FP8X4),
-                lhsT_scale=w_sc[d][:, 128 * t : 128 * (t + 1)],
+                lhsT_scale=w_sc[d][:, P * t : P * (t + 1)],
                 rhs=x_codes[d][:, v0:v1].bitcast(FP4X4),
                 rhs_scale=x_sc[d][:, v0:v1],
                 start=True,
                 stop=True,
             )
 
-        def first(t):
-            nc.scalar.copy(p1_of[t], y1_of[t])
+        def copy_y1(t):
+            nc.scalar.copy(y1_sbuf[t], y1[t])
 
-        def second(t):
-            nc.vector.tensor_tensor(p12[:, V * t : V * (t + 1)], y2_of[t], p1_of[t], MULT)
+        def multiply_y12(t):
+            nc.vector.tensor_tensor(y12[:, V * t : V * (t + 1)], y2[t], y1_sbuf[t], MULT)
 
-        def third(h):
+        def make_z(h):
             nc.vector.tensor_tensor(
-                last_in[:, 512 * (h + 1) : 512 * (h + 2)].rearrange("p (c e t) -> p c t e", e=2, t=4),
+                last_in[:, 4 * (N + HALF * h) : 4 * (N + HALF * (h + 1))].rearrange("p (c e t) -> p c t e", e=2, t=4),
                 y3[h][:].rearrange("p t (c e) -> p c t e", e=2),
-                p12.rearrange("p (t c e) -> p c t e", t=4, e=2)[:, 64 * h : 64 * (h + 1)],
+                y12.rearrange("p (t c e) -> p c t e", t=4, e=2)[:, HALF // 2 * h : HALF // 2 * (h + 1)],
                 MULT,
             )
 
-        def weave4():
-            nc.scalar.copy(last_in[:, 0:512].rearrange("p (c i t) -> p c t i", i=2, t=4), raw4[:].rearrange("p t (c i) -> p c t i", i=2))
-
-        def quant_last(c0, c1):
+        def quantise_last(c0, c1):
             nc.vector.quantize_mx(last_codes[:, c0:c1].bitcast(FP8X4), last_sc[:, c0:c1], last_in[:, 4 * c0 : 4 * c1])
 
-        def last(h):
-            acc = psum.tile([P, 128], F32, name="acc%d" % h, tag="single%d" % h)
+        def last_product(h):
+            acc = psum.tile([P, HALF], F32, name="acc%d" % h, tag="single%d" % h)
+            z_cols = slice(N + HALF * h, N + HALF * (h + 1))
             nc.tensor.matmul_mx(
                 acc[:],
-                lhsT=last_codes[:, 0:128].bitcast(FP8X4),
-                lhsT_scale=last_sc[:, 0:128],
-                rhs=last_codes[:, 128 * (h + 1) : 128 * (h + 2)].bitcast(FP8X4),
-                rhs_scale=last_sc[:, 128 * (h + 1) : 128 * (h + 2)],
+                lhsT=last_codes[:, 0:N].bitcast(FP8X4),
+                lhsT_scale=last_sc[:, 0:N],
+                rhs=last_codes[:, z_cols].bitcast(FP8X4),
+                rhs_scale=last_sc[:, z_cols],
                 start=True,
                 stop=True,
             )
-            nc.scalar.activation(res[h][:], acc[:], RELU)
+            nc.scalar.activation(res[:, HALF * h : HALF * (h + 1)], acc[:], RELU)
 
-        on_scalar, on_vector = nc.scalar.copy, nc.vector.tensor_copy
-        weave_first_rows()
+        src = raw[0][:].rearrange("p (j q t r) -> p t q j r", j=4, t=4, r=2)[:, 0:3, :, 0:2]
+        on_scalar(woven1[:].rearrange("p (t q r j) -> p t q j r", t=4, r=2, j=4)[:, 0:3, :, 0:2], src)
         for t in range(3):
-            weave(on_scalar, 0, t, 0, 64, 2, 4)
-        quant(0, 0)
-        quant(0, 1)
-        weave(on_scalar, 0, 3, 0, 64)
-        quant(0, 2)
+            weave(on_scalar, 0, t, 0, Q, 2, 4)
+        quantise(0, 0)
+        quantise(0, 1)
+        weave(on_scalar, 0, 3, 0, Q)
+        quantise(0, 2)
         for t in range(3):
-            product(y1_of[t], 0, t, 0, V)
-        weave(on_scalar, 1, 2, 16, 32)
-        weave(on_scalar, 1, 3, 0, 32)
-        weave(on_scalar, 1, 2, 32, 64)
-        weave(on_scalar, 1, 3, 32, 64)
-        weave_lower(1, 0, 32)
-        weave(on_vector, 1, 0, 32, 64)
-        weave(on_vector, 1, 1, 32, 64)
-        weave(on_vector, 1, 2, 0, 16)
+            product(y1[t], 0, t, 0, V)
+
+        weave_shared(1)
         for t in range(4):
-            quant(1, t)
+            quantise(1, t)
         for t in range(4):
-            product(y2_of[t], 1, t, 0, V)
-        codes[0, 3] = keep.tile([P, 128], U32, name="codes_late", tag="lower2", align_bytes=64)[:]
-        quant(0, 3)
-        product(y1_of[3], 0, 3, 0, V)
+            product(y2[t], 1, t, 0, V)
+        codes[0, 3] = keep.tile([P, P], U32, name="codes_late", tag="lower2", align_bytes=64)[:]
+        quantise(0, 3)
+        product(y1[3], 0, 3, 0, V)
         for t in range(3):
-            first(t)
-        second(0)
-        second(1)
-        weave(on_scalar, 2, 2, 16, 32)
-        weave(on_scalar, 2, 3, 0, 32)
-        weave(on_scalar, 2, 2, 32, 64)
-        weave(on_scalar, 2, 3, 32, 64)
-        weave_lower(2, 0, 32)
-        weave(on_vector, 2, 0, 32, 64)
-        weave(on_vector, 2, 1, 32, 64)
-        weave(on_vector, 2, 2, 0, 16)
+            copy_y1(t)
+        multiply_y12(0)
+        multiply_y12(1)
+
+        weave_shared(2)
         for t in range(4):
-            quant(2, t)
-        first(3)
+            quantise(2, t)
+        copy_y1(3)
         for h in range(2):
-            y3.append(psum.tile([P, 4, 128], F32, name="y3_%d" % h, tag="bank%d" % h))
+            y3.append(psum.tile([P, 4, HALF], F32, name="y3_%d" % h, tag="bank%d" % h))
             for t in range(4):
-                product(y3[h][:, t, :], 2, t, 128 * h, 128 * (h + 1))
-        weave4()
-        second(2)
-        second(3)
-        third(0)
-        third(1)
-        quant_last(0, 256)
-        last(0)
-        quant_last(256, 384)
-        last(1)
-        for h in range(2):
-            nc.scalar.dma_start(out[:, 128 * h : 128 * (h + 1)], res[h][:])
+                product(y3[h][:, t, :], 2, t, HALF * h, HALF * (h + 1))
+        on_scalar(
+            last_in[:, 0 : 4 * N].rearrange("p (c e t) -> p c t e", e=2, t=4),
+            raw4[:].rearrange("p t (c e) -> p c t e", e=2),
+        )
+        multiply_y12(2)
+        multiply_y12(3)
+        make_z(0)
+        make_z(1)
+        quantise_last(0, N + HALF)
+        last_product(0)
+        quantise_last(N + HALF, N + V)
+        last_product(1)
+        nc.scalar.dma_start(out, res[:])

@@ -133,9 +133,9 @@ def tile_picked_trilin_relu_p_kernel(tc, x_words, x_scales, w1, w2, w3, w4, offs
 
         def make_z(h):
             nc.vector.tensor_tensor(
-                last_in[:, 4 * (N + HALF * h) : 4 * (N + HALF * (h + 1))].rearrange("p (c e t) -> p c t e", e=2, t=4),
-                y3[h][:].rearrange("p t (c e) -> p c t e", e=2),
-                y12.rearrange("p (t c e) -> p c t e", t=4, e=2)[:, HALF // 2 * h : HALF // 2 * (h + 1)],
+                last_in[:, 4 * (N + HALF * h) : 4 * (N + HALF * (h + 1))].rearrange("p (c e t) -> p c t e", e=4, t=4),
+                y3[h][:].rearrange("p t (c e) -> p c t e", e=4),
+                y12.rearrange("p (t c e) -> p c t e", t=4, e=4)[:, HALF // 4 * h : HALF // 4 * (h + 1)],
                 MULT,
             )
 
@@ -189,8 +189,8 @@ def tile_picked_trilin_relu_p_kernel(tc, x_words, x_scales, w1, w2, w3, w4, offs
             for t in range(4):
                 product(y3[h][:, t, :], 2, t, HALF * h, HALF * (h + 1))
         on_scalar(
-            last_in[:, 0 : 4 * N].rearrange("p (c e t) -> p c t e", e=2, t=4),
-            raw4[:].rearrange("p t (c e) -> p c t e", e=2),
+            last_in[:, 0 : 4 * N].rearrange("p (c e t) -> p c t e", e=4, t=4),
+            raw4[:].rearrange("p t (c e) -> p c t e", e=4),
         )
         multiply_y12(2)
         multiply_y12(3)

@@ -66,9 +66,8 @@ def tile_picked_trilin_relu_p_kernel(tc, x_words, x_scales, w1, w2, w3, w4, offs
         w_sc = [keep.tile([P, H], U8, name="w_sc%d" % d, align_bytes=64) for d in range(3)]
 
         y1_01 = psum.tile([P, 2 * V], F32, name="y1_01", tag="bank0")
-        y1_2 = psum.tile([P, V], F32, name="y1_2")
-        y1_3 = psum.tile([P, V], F32, name="y1_3", tag="bank1")
-        y1 = [y1_01[:, 0:V], y1_01[:, V : 2 * V], y1_2[:], y1_3[:]]
+        y1_23 = psum.tile([P, 2 * V], F32, name="y1_23", tag="bank1")
+        y1 = [y1_01[:, 0:V], y1_01[:, V : 2 * V], y1_23[:, 0:V], y1_23[:, V : 2 * V]]
         y2_0 = psum.tile([P, V], F32, name="y2_0", tag="single0")
         y2_1 = psum.tile([P, V], F32, name="y2_1", tag="single1")
         y2_23 = psum.tile([P, 2 * V], F32, name="y2_23")
@@ -80,7 +79,8 @@ def tile_picked_trilin_relu_p_kernel(tc, x_words, x_scales, w1, w2, w3, w4, offs
         upper2 = keep.tile([P, 2 * GROUP], BF16, name="upper2", align_bytes=64)
         arena = keep.tile([P, 5 * V], F32, name="arena", align_bytes=64)
         y12 = arena[:, 0 : 4 * V]
-        y1_sbuf = [raw[1][:, H * (t % 3) : H * (t % 3) + V] for t in range(4)]
+        y1_sbuf = raw[1][:].rearrange("p (t c) -> p t c", t=4)[:, :, 0:V]
+        y1_upper = raw[2][:].rearrange("p (t c) -> p t c", t=4)[:, 0:2, V : 2 * V]
         lower = {1: lower2[:], 2: raw[1][:, 0:H].bitcast(BF16)}
         groups = {(0, t): woven1[:, GROUP * t : GROUP * (t + 1)] for t in range(4)}
         for t in range(4):
@@ -126,10 +126,19 @@ def tile_picked_trilin_relu_p_kernel(tc, x_words, x_scales, w1, w2, w3, w4, offs
             )
 
         def copy_y1(t):
-            nc.scalar.copy(y1_sbuf[t], y1[t])
+            nc.scalar.copy(y1_sbuf[:, t], y1[t])
 
         def multiply_y12(t):
-            nc.vector.tensor_tensor(y12[:, V * t : V * (t + 1)], y2[t], y1_sbuf[t], MULT)
+            nc.vector.tensor_tensor(y12[:, V * t : V * (t + 1)], y2[t], y1_sbuf[:, t], MULT)
+
+        def multiply_upper(h):
+            v = slice(HALF * h, HALF * (h + 1))
+            nc.vector.tensor_tensor(
+                y12.rearrange("p (t v) -> p t v", t=4)[:, 2:4, v],
+                y2_23[:].rearrange("p (t v) -> p t v", t=2)[:, :, v],
+                y1_upper[:, :, v],
+                MULT,
+            )
 
         def make_z(h):
             nc.vector.tensor_tensor(
@@ -175,7 +184,7 @@ def tile_picked_trilin_relu_p_kernel(tc, x_words, x_scales, w1, w2, w3, w4, offs
         codes[0, 3] = keep.tile([P, P], U32, name="codes_late", tag="lower2", align_bytes=64)[:]
         quantise(0, 3)
         product(y1[3], 0, 3, 0, V)
-        for t in range(3):
+        for t in range(2):
             copy_y1(t)
         multiply_y12(0)
         multiply_y12(1)
@@ -183,7 +192,9 @@ def tile_picked_trilin_relu_p_kernel(tc, x_words, x_scales, w1, w2, w3, w4, offs
         weave_shared(2)
         for t in range(4):
             quantise(2, t)
-        copy_y1(3)
+        for h in range(2):
+            v = slice(HALF * h, HALF * (h + 1))
+            nc.scalar.copy(y1_upper[:, :, v], y1_23[:].rearrange("p (t v) -> p t v", t=2)[:, :, v])
         for h in range(2):
             y3.append(psum.tile([P, 4, HALF], F32, name="y3_%d" % h, tag="bank%d" % h))
             for t in range(4):
@@ -192,8 +203,8 @@ def tile_picked_trilin_relu_p_kernel(tc, x_words, x_scales, w1, w2, w3, w4, offs
             last_in[:, 0 : 4 * N].rearrange("p (c e t) -> p c t e", e=4, t=4),
             raw4[:].rearrange("p t (c e) -> p c t e", e=4),
         )
-        multiply_y12(2)
-        multiply_y12(3)
+        multiply_upper(0)
+        multiply_upper(1)
         make_z(0)
         make_z(1)
         quantise_last(0, N + HALF)

@@ -19,10 +19,10 @@ RELU = mybir.ActivationFunctionType.Relu
 P = 128
 GROUP = 4 * P
 HALF = V // 2
-Q = H // 8
+Q = H // 16
 LIST_COLS = V // 16
 CUT = 3 * H + H // 2
-Q_VECTOR = 16
+Q_VECTOR = 8
 
 
 def tile_picked_trilin_relu_p_kernel(tc, x_words, x_scales, w1, w2, w3, w4, offs, out):
@@ -46,12 +46,12 @@ def tile_picked_trilin_relu_p_kernel(tc, x_words, x_scales, w1, w2, w3, w4, offs
                 x_scales[0, 4 * quadrant : 4 * quadrant + 4, :].bitcast(I32),
             )
         nc.sync.dma_start(raw[0][:, 2 * H : 4 * H], rows[0][:, 2 * H : 4 * H])
-        for d in (1, 2):
-            for c0, c1 in ((0, CUT), (CUT, 4 * H)):
-                nc.sync.dma_start(raw[d][:, c0:c1], rows[d][:, c0:c1])
-        raw4 = keep.tile([P, 4, N], F32, name="raw4", align_bytes=64)
-        for r in range(2):
-            nc.sync.dma_start(raw4[r:P:2, :, :], w4.rearrange("(q t r) n -> r q t n", t=4, r=2)[r])
+        nc.sync.dma_start(raw[1][:], rows[1])
+        for c0, c1 in ((0, CUT), (CUT, 4 * H)):
+            nc.sync.dma_start(raw[2][:, c0:c1], rows[2][:, c0:c1])
+        raw4 = keep.tile([P, 4, N], F32, name="raw4", tag="raw4", align_bytes=64)
+        for t in range(4):
+            nc.sync.dma_start(raw4[:, t, :], w4.rearrange("(q t r) n -> t q r n", t=4, r=4)[t])
 
         words01 = keep.tile([P, 2 * V], U16, name="words01", align_bytes=64)
         words2 = keep.tile([P, V], U16, name="words2", align_bytes=64)
@@ -90,23 +90,22 @@ def tile_picked_trilin_relu_p_kernel(tc, x_words, x_scales, w1, w2, w3, w4, offs
         codes = {(d, t): w_codes[d][:, P * t : P * (t + 1)] for d in range(3) for t in range(4)}
 
         last_in = keep.tile([P, 4 * (N + V)], BF16, name="last_in", align_bytes=64)
-        last_codes = keep.tile([P, N + V], U32, name="last_codes", align_bytes=64)
         last_sc = keep.tile([P, N + V], U8, name="last_sc", align_bytes=64)
         res = keep.tile([P, V], F32, name="res")
 
         on_scalar, on_vector = nc.scalar.copy, nc.vector.tensor_copy
 
         def weave(copy, d, t, q0, q1, j0=0, j1=4):
-            src = raw[d][:].rearrange("p (j q t r) -> p t q j r", j=4, t=4, r=2)[:, t, q0:q1, j0:j1]
-            copy(groups[d, t].rearrange("p (q r j) -> p q j r", r=2, j=4)[:, q0:q1, j0:j1], src)
+            src = raw[d][:].rearrange("p (j q t r) -> p t q j r", j=4, t=4, r=4)[:, t, q0:q1, j0:j1]
+            copy(groups[d, t].rearrange("p (q r j) -> p q j r", r=4, j=4)[:, q0:q1, j0:j1], src)
 
         def weave_shared(d):
             weave(on_scalar, d, 2, Q_VECTOR, Q // 2)
             weave(on_scalar, d, 3, 0, Q // 2)
             weave(on_scalar, d, 2, Q // 2, Q)
             weave(on_scalar, d, 3, Q // 2, Q)
-            src = raw[d][:].rearrange("p (j q t r) -> p t q j r", j=4, t=4, r=2)[:, 0:2, 0 : Q // 2]
-            on_vector(lower[d].rearrange("p (t q r j) -> p t q j r", t=2, r=2, j=4)[:, :, 0 : Q // 2], src)
+            src = raw[d][:].rearrange("p (j q t r) -> p t q j r", j=4, t=4, r=4)[:, 0:2, 0 : Q // 2]
+            on_vector(lower[d].rearrange("p (t q r j) -> p t q j r", t=2, r=4, j=4)[:, :, 0 : Q // 2], src)
             weave(on_vector, d, 0, Q // 2, Q)
             weave(on_vector, d, 1, Q // 2, Q)
             weave(on_vector, d, 2, 0, Q_VECTOR)
@@ -165,8 +164,8 @@ def tile_picked_trilin_relu_p_kernel(tc, x_words, x_scales, w1, w2, w3, w4, offs
             )
             nc.scalar.activation(res[:, HALF * h : HALF * (h + 1)], acc[:], RELU)
 
-        src = raw[0][:].rearrange("p (j q t r) -> p t q j r", j=4, t=4, r=2)[:, 0:3, :, 0:2]
-        on_scalar(woven1[:].rearrange("p (t q r j) -> p t q j r", t=4, r=2, j=4)[:, 0:3, :, 0:2], src)
+        src = raw[0][:].rearrange("p (j q t r) -> p t q j r", j=4, t=4, r=4)[:, 0:3, :, 0:2]
+        on_scalar(woven1[:].rearrange("p (t q r j) -> p t q j r", t=4, r=4, j=4)[:, 0:3, :, 0:2], src)
         for t in range(3):
             weave(on_scalar, 0, t, 0, Q, 2, 4)
         quantise(0, 0)
@@ -203,6 +202,7 @@ def tile_picked_trilin_relu_p_kernel(tc, x_words, x_scales, w1, w2, w3, w4, offs
             last_in[:, 0 : 4 * N].rearrange("p (c e t) -> p c t e", e=4, t=4),
             raw4[:].rearrange("p t (c e) -> p c t e", e=4),
         )
+        last_codes = keep.tile([P, N + V], U32, name="last_codes", tag="raw4", align_bytes=64)
         multiply_upper(0)
         multiply_upper(1)
         make_z(0)

@@ -174,6 +174,16 @@ def tile_picked_trilin_relu_p_kernel(tc, x_words, x_scales, w1, w2, w3, w4, offs
         quantise(0, 2)
         for t in range(3):
             product(y1[t], 0, t, 0, V)
+        warm = psum.tile([P, V], F32, name="warm")
+        nc.tensor.matmul_mx(
+            warm[:],
+            lhsT=codes[0, 2].bitcast(FP8X4),
+            lhsT_scale=w_sc[0][:, 2 * P : 3 * P],
+            rhs=w_codes[0][:, 0 : 2 * P].bitcast(FP8X4),
+            rhs_scale=w_sc[0][:, 0 : 2 * P],
+            start=True,
+            stop=True,
+        )
 
         weave_shared(1)
         for t in range(4):

@@ -66,8 +66,8 @@ def tile_picked_trilin_relu_p_kernel(tc, x_words, x_scales, w1, w2, w3, w4, offs
         w_sc = [keep.tile([P, H], U8, name="w_sc%d" % d, align_bytes=64) for d in range(3)]
 
         y1_01 = psum.tile([P, 2 * V], F32, name="y1_01", tag="bank0")
-        y1_23 = psum.tile([P, 2 * V], F32, name="y1_23", tag="bank1")
-        y1 = [y1_01[:, 0:V], y1_01[:, V : 2 * V], y1_23[:, 0:V], y1_23[:, V : 2 * V]]
+        y1 = [y1_01[:, 0:V], y1_01[:, V : 2 * V]]
+        y1_23 = [psum.tile([P, 2, HALF], F32, name="y1_23_%d" % h, tag="bank%d" % (h + 1)) for h in range(2)]
         y2_0 = psum.tile([P, V], F32, name="y2_0", tag="single0")
         y2_1 = psum.tile([P, V], F32, name="y2_1", tag="single1")
         y2_23 = psum.tile([P, 2 * V], F32, name="y2_23")
@@ -124,6 +124,10 @@ def tile_picked_trilin_relu_p_kernel(tc, x_words, x_scales, w1, w2, w3, w4, offs
                 stop=True,
             )
 
+        def product_upper(t):
+            for h in range(2):
+                product(y1_23[h][:, t - 2, :], 0, t, HALF * h, HALF * (h + 1))
+
         def copy_y1(t):
             nc.scalar.copy(y1_sbuf[:, t], y1[t])
 
@@ -172,8 +176,9 @@ def tile_picked_trilin_relu_p_kernel(tc, x_words, x_scales, w1, w2, w3, w4, offs
         quantise(0, 1)
         weave(on_scalar, 0, 3, 0, Q)
         quantise(0, 2)
-        for t in range(3):
+        for t in range(2):
             product(y1[t], 0, t, 0, V)
+        product_upper(2)
         warm = psum.tile([P, V], F32, name="warm")
         nc.tensor.matmul_mx(
             warm[:],
@@ -192,7 +197,7 @@ def tile_picked_trilin_relu_p_kernel(tc, x_words, x_scales, w1, w2, w3, w4, offs
             product(y2[t], 1, t, 0, V)
         codes[0, 3] = keep.tile([P, P], U32, name="codes_late", tag="lower2", align_bytes=64)[:]
         quantise(0, 3)
-        product(y1[3], 0, 3, 0, V)
+        product_upper(3)
         for t in range(2):
             copy_y1(t)
         multiply_y12(0)
@@ -203,7 +208,7 @@ def tile_picked_trilin_relu_p_kernel(tc, x_words, x_scales, w1, w2, w3, w4, offs
             quantise(2, t)
         for h in range(2):
             v = slice(HALF * h, HALF * (h + 1))
-            nc.scalar.copy(y1_upper[:, :, v], y1_23[:].rearrange("p (t v) -> p t v", t=2)[:, :, v])
+            nc.scalar.copy(y1_upper[:, :, v], y1_23[h][:])
         for h in range(2):
             y3.append(psum.tile([P, 4, HALF], F32, name="y3_%d" % h, tag="bank%d" % h))
             for t in range(4):

@@ -22,7 +22,7 @@ HALF = V // 2
 Q = H // 16
 LIST_COLS = V // 16
 CUT = 3 * H + H // 2
-Q_VECTOR = 8
+DMA_ALIGN = 256
 
 
 def tile_picked_trilin_relu_p_kernel(tc, x_words, x_scales, w1, w2, w3, w4, offs, out):
@@ -31,13 +31,15 @@ def tile_picked_trilin_relu_p_kernel(tc, x_words, x_scales, w1, w2, w3, w4, offs
         keep = ctx.enter_context(tc.tile_pool(name="keep", bufs=1))
         psum = ctx.enter_context(tc.psum_pool(name="psum", bufs=1))
 
-        scale_table = keep.tile([P, T], U8, name="scale_table", align_bytes=64)
+        scale_table = keep.tile([P, T], U8, name="scale_table", align_bytes=DMA_ALIGN)
         nc.vector.memset(scale_table[:].bitcast(I32), 0)
-        word_table = keep.tile([P, T], U16, name="word_table", align_bytes=64)
-        offsets = keep.tile([P, 3 * LIST_COLS], U16, name="offsets")
+        word_table = keep.tile([P, T], U16, name="word_table", align_bytes=DMA_ALIGN)
+        offsets = keep.tile([P, 3 * LIST_COLS], U16, name="offsets", align_bytes=DMA_ALIGN)
         nc.sync.dma_start(word_table[:].bitcast(I32), x_words[0].bitcast(I32))
         nc.sync.dma_start(offsets[:], offs)
-        raw = [keep.tile([P, 4 * H], F32, name="raw%d" % d, align_bytes=64) for d in range(3)]
+        raw = [keep.tile([P, 4 * H], F32, name="raw%d" % d, align_bytes=DMA_ALIGN)[:] for d in range(2)]
+        arena = keep.tile([P, 5 * H], F32, name="arena", align_bytes=DMA_ALIGN)
+        raw.append(arena[:, H : 5 * H])
         rows = [w.rearrange("(p j) c -> p (j c)", j=4) for w in (w1, w2, w3)]
         nc.sync.dma_start(raw[0][:, 0 : 2 * H], rows[0][:, 0 : 2 * H])
         for quadrant in range(4):
@@ -46,12 +48,13 @@ def tile_picked_trilin_relu_p_kernel(tc, x_words, x_scales, w1, w2, w3, w4, offs
                 x_scales[0, 4 * quadrant : 4 * quadrant + 4, :].bitcast(I32),
             )
         nc.sync.dma_start(raw[0][:, 2 * H : 4 * H], rows[0][:, 2 * H : 4 * H])
-        nc.sync.dma_start(raw[1][:], rows[1])
+        nc.sync.dma_start(raw[1], rows[1])
         for c0, c1 in ((0, CUT), (CUT, 4 * H)):
             nc.sync.dma_start(raw[2][:, c0:c1], rows[2][:, c0:c1])
-        raw4 = keep.tile([P, 4, N], F32, name="raw4", tag="raw4", align_bytes=64)
-        for t in range(4):
-            nc.sync.dma_start(raw4[:, t, :], w4.rearrange("(q t r) n -> t q r n", t=4, r=4)[t])
+        raw4 = keep.tile([P, 4 * N], F32, name="raw4", tag="raw4", align_bytes=DMA_ALIGN)
+        for t in range(2):
+            nc.sync.dma_start(raw4[:, N * t : N * (t + 1)], w4.rearrange("(q s r) n -> s q r n", s=4, r=4)[t])
+        nc.sync.dma_start(raw4[:, 2 * N : 4 * N], w4.rearrange("(q u r e) n -> u q r (e n)", u=2, r=4, e=2)[1])
 
         words01 = keep.tile([P, 2 * V], U16, name="words01", align_bytes=64)
         words2 = keep.tile([P, V], U16, name="words2", align_bytes=64)
@@ -62,61 +65,58 @@ def tile_picked_trilin_relu_p_kernel(tc, x_words, x_scales, w1, w2, w3, w4, offs
         x_codes = [words01[:, 0:V], words01[:, V : 2 * V], words2[:]]
         x_sc = [picked_scales[:, V * d : V * (d + 1)] for d in range(3)]
 
+        woven1 = keep.tile([P, 4 * GROUP], BF16, name="woven1", align_bytes=64)
+        woven2_0 = keep.tile([P, GROUP], BF16, name="woven2_0", tag="woven2_0", align_bytes=64)
+        woven2_rest = keep.tile([P, 3 * GROUP], BF16, name="woven2_rest", align_bytes=64)
+        woven3_pair = keep.tile([P, 2 * GROUP], BF16, name="woven3_pair", align_bytes=64)
+        woven = {
+            (0, 0): woven1[:, 0 : 2 * GROUP],
+            (0, 1): woven1[:, 2 * GROUP : 4 * GROUP],
+            (1, 1): woven2_rest[:, GROUP : 3 * GROUP],
+            (2, 0): raw[1][:, 0:H].bitcast(BF16),
+            (2, 1): woven3_pair[:],
+        }
+        y12 = arena[:, 0 : 4 * H].rearrange("p (t c) -> p t c", t=4)[:, :, 0:V]
+        y1_lower = raw[1].rearrange("p (t c) -> p t c", t=4)[:, 0:2, 0:V]
+        y1_upper = raw[2].rearrange("p (t c) -> p t c", t=4)[:, 0:2, V : 2 * V]
+
         w_codes = [keep.tile([P, H], U32, name="w_codes%d" % d, align_bytes=64) for d in range(3)]
         w_sc = [keep.tile([P, H], U8, name="w_sc%d" % d, align_bytes=64) for d in range(3)]
+        codes = {(d, u): w_codes[d][:, 2 * P * u : 2 * P * (u + 1)] for d in range(3) for u in range(2)}
 
-        y1_01 = psum.tile([P, 2 * V], F32, name="y1_01", tag="bank0")
-        y1 = [y1_01[:, 0:V], y1_01[:, V : 2 * V]]
-        y1_23 = [psum.tile([P, 2, HALF], F32, name="y1_23_%d" % h, tag="bank%d" % (h + 1)) for h in range(2)]
-        y2_0 = psum.tile([P, V], F32, name="y2_0", tag="single0")
-        y2_1 = psum.tile([P, V], F32, name="y2_1", tag="single1")
-        y2_23 = psum.tile([P, 2 * V], F32, name="y2_23")
-        y2 = [y2_0[:], y2_1[:], y2_23[:, 0:V], y2_23[:, V : 2 * V]]
+        y1_01 = psum.tile([P, 2, V], F32, name="y1_01", tag="bank0")
+        y1_23 = psum.tile([P, 2, V], F32, name="y1_23")
+        y2 = [psum.tile([P, V], F32, name="y2_%d" % t, tag="single%d" % t) for t in range(2)]
+        y2_23 = [psum.tile([P, 2, HALF], F32, name="y2_23_%d" % h, tag="half%d" % h) for h in range(2)]
         y3 = []
-
-        woven1 = keep.tile([P, 4 * GROUP], BF16, name="woven1", align_bytes=64)
-        lower2 = keep.tile([P, 2 * GROUP], BF16, name="lower2", tag="lower2", align_bytes=64)
-        upper2 = keep.tile([P, 2 * GROUP], BF16, name="upper2", align_bytes=64)
-        arena = keep.tile([P, 5 * V], F32, name="arena", align_bytes=64)
-        y12 = arena[:, 0 : 4 * V]
-        y1_sbuf = raw[1][:].rearrange("p (t c) -> p t c", t=4)[:, :, 0:V]
-        y1_upper = raw[2][:].rearrange("p (t c) -> p t c", t=4)[:, 0:2, V : 2 * V]
-        lower = {1: lower2[:], 2: raw[1][:, 0:H].bitcast(BF16)}
-        groups = {(0, t): woven1[:, GROUP * t : GROUP * (t + 1)] for t in range(4)}
-        for t in range(4):
-            groups[1, t] = (lower2, upper2)[t // 2][:, GROUP * (t % 2) : GROUP * (t % 2 + 1)]
-        groups[2, 0], groups[2, 1] = lower[2][:, 0:GROUP], lower[2][:, GROUP : 2 * GROUP]
-        groups[2, 2], groups[2, 3] = arena[:, 2 * V : 3 * V].bitcast(BF16), arena[:, 4 * V : 5 * V].bitcast(BF16)
-        codes = {(d, t): w_codes[d][:, P * t : P * (t + 1)] for d in range(3) for t in range(4)}
 
         last_in = keep.tile([P, 4 * (N + V)], BF16, name="last_in", align_bytes=64)
         last_sc = keep.tile([P, N + V], U8, name="last_sc", align_bytes=64)
-        res = keep.tile([P, V], F32, name="res")
+        res = keep.tile([P, V], F32, name="res", align_bytes=DMA_ALIGN)
 
         on_scalar, on_vector = nc.scalar.copy, nc.vector.tensor_copy
 
-        def weave(copy, d, t, q0, q1, j0=0, j1=4):
-            src = raw[d][:].rearrange("p (j q t r) -> p t q j r", j=4, t=4, r=4)[:, t, q0:q1, j0:j1]
-            copy(groups[d, t].rearrange("p (q r j) -> p q j r", r=4, j=4)[:, q0:q1, j0:j1], src)
+        def weave_group(copy, dst, d, t):
+            src = raw[d].rearrange("p (j q s r) -> p s q j r", j=4, s=4, r=4)[:, t]
+            copy(dst.rearrange("p (q r j) -> p q j r", r=4, j=4), src)
 
-        def weave_shared(d):
-            weave(on_scalar, d, 2, Q_VECTOR, Q // 2)
-            weave(on_scalar, d, 3, 0, Q // 2)
-            weave(on_scalar, d, 2, Q // 2, Q)
-            weave(on_scalar, d, 3, Q // 2, Q)
-            src = raw[d][:].rearrange("p (j q t r) -> p t q j r", j=4, t=4, r=4)[:, 0:2, 0 : Q // 2]
-            on_vector(lower[d].rearrange("p (t q r j) -> p t q j r", t=2, r=4, j=4)[:, :, 0 : Q // 2], src)
-            weave(on_vector, d, 0, Q // 2, Q)
-            weave(on_vector, d, 1, Q // 2, Q)
-            weave(on_vector, d, 2, 0, Q_VECTOR)
+        def weave_lower(copy, d, q0, q1, j0=0, j1=4):
+            src = raw[d].rearrange("p (j q s r) -> p s q j r", j=4, s=4, r=4)[:, 0:2, q0:q1, j0:j1]
+            copy(woven[d, 0].rearrange("p (t q r j) -> p t q j r", t=2, r=4, j=4)[:, :, q0:q1, j0:j1], src)
 
-        def quantise(d, t):
-            nc.vector.quantize_mx(codes[d, t].bitcast(FP8X4), w_sc[d][:, P * t : P * (t + 1)], groups[d, t])
+        def weave_pair(copy, d, q0, q1, j0=0, j1=4):
+            src = raw[d].rearrange("p (j q u h r e) -> p u q h j r e", j=4, u=2, h=2, r=2, e=2)[:, 1, q0:q1, :, j0:j1]
+            dst = woven[d, 1].rearrange("p (e q h r j) -> p q h j r e", e=2, h=2, r=2, j=4)
+            copy(dst[:, q0:q1, :, j0:j1], src)
+
+        def quantise(d, t0, t1, src):
+            u, c0, c1 = t0 // 2, P * (t0 % 2), P * (t1 - t0 + t0 % 2)
+            nc.vector.quantize_mx(codes[d, u][:, c0:c1].bitcast(FP8X4), w_sc[d][:, P * t0 : P * t1], src)
 
         def product(bank, d, t, v0, v1):
             nc.tensor.matmul_mx(
                 bank,
-                lhsT=codes[d, t].bitcast(FP8X4),
+                lhsT=codes[d, t // 2][:, P * (t % 2) : P * (t % 2 + 1)].bitcast(FP8X4),
                 lhsT_scale=w_sc[d][:, P * t : P * (t + 1)],
                 rhs=x_codes[d][:, v0:v1].bitcast(FP4X4),
                 rhs_scale=x_sc[d][:, v0:v1],
@@ -124,30 +124,18 @@ def tile_picked_trilin_relu_p_kernel(tc, x_words, x_scales, w1, w2, w3, w4, offs
                 stop=True,
             )
 
-        def product_upper(t):
-            for h in range(2):
-                product(y1_23[h][:, t - 2, :], 0, t, HALF * h, HALF * (h + 1))
-
-        def copy_y1(t):
-            nc.scalar.copy(y1_sbuf[:, t], y1[t])
-
-        def multiply_y12(t):
-            nc.vector.tensor_tensor(y12[:, V * t : V * (t + 1)], y2[t], y1_sbuf[:, t], MULT)
+        def multiply_lower(t):
+            nc.vector.tensor_tensor(y12[:, t], y2[t][:], y1_lower[:, t], MULT)
 
         def multiply_upper(h):
             v = slice(HALF * h, HALF * (h + 1))
-            nc.vector.tensor_tensor(
-                y12.rearrange("p (t v) -> p t v", t=4)[:, 2:4, v],
-                y2_23[:].rearrange("p (t v) -> p t v", t=2)[:, :, v],
-                y1_upper[:, :, v],
-                MULT,
-            )
+            nc.vector.tensor_tensor(y12[:, 2:4, v], y2_23[h][:], y1_upper[:, :, v], MULT)
 
         def make_z(h):
             nc.vector.tensor_tensor(
                 last_in[:, 4 * (N + HALF * h) : 4 * (N + HALF * (h + 1))].rearrange("p (c e t) -> p c t e", e=4, t=4),
                 y3[h][:].rearrange("p t (c e) -> p c t e", e=4),
-                y12.rearrange("p (t c e) -> p c t e", t=4, e=4)[:, HALF // 4 * h : HALF // 4 * (h + 1)],
+                y12[:, :, HALF * h : HALF * (h + 1)].rearrange("p t (c e) -> p c t e", e=4),
                 MULT,
             )
 
@@ -168,57 +156,56 @@ def tile_picked_trilin_relu_p_kernel(tc, x_words, x_scales, w1, w2, w3, w4, offs
             )
             nc.scalar.activation(res[:, HALF * h : HALF * (h + 1)], acc[:], RELU)
 
-        src = raw[0][:].rearrange("p (j q t r) -> p t q j r", j=4, t=4, r=4)[:, 0:3, :, 0:2]
-        on_scalar(woven1[:].rearrange("p (t q r j) -> p t q j r", t=4, r=4, j=4)[:, 0:3, :, 0:2], src)
-        for t in range(3):
-            weave(on_scalar, 0, t, 0, Q, 2, 4)
-        quantise(0, 0)
-        quantise(0, 1)
-        weave(on_scalar, 0, 3, 0, Q)
-        quantise(0, 2)
+        weave_lower(on_scalar, 0, 0, Q, 0, 2)
+        weave_pair(on_scalar, 0, 0, Q // 2, 0, 2)
+        weave_lower(on_scalar, 0, 0, Q, 2, 4)
+        weave_pair(on_scalar, 0, 0, Q // 2, 2, 4)
+        weave_pair(on_scalar, 0, Q // 2, Q)
+        quantise(0, 0, 2, woven[0, 0])
         for t in range(2):
-            product(y1[t], 0, t, 0, V)
-        product_upper(2)
-        warm = psum.tile([P, V], F32, name="warm")
-        nc.tensor.matmul_mx(
-            warm[:],
-            lhsT=codes[0, 2].bitcast(FP8X4),
-            lhsT_scale=w_sc[0][:, 2 * P : 3 * P],
-            rhs=w_codes[0][:, 0 : 2 * P].bitcast(FP8X4),
-            rhs_scale=w_sc[0][:, 0 : 2 * P],
-            start=True,
-            stop=True,
-        )
+            product(y1_01[:, t, :], 0, t, 0, V)
 
-        weave_shared(1)
-        for t in range(4):
-            quantise(1, t)
-        for t in range(4):
-            product(y2[t], 1, t, 0, V)
-        codes[0, 3] = keep.tile([P, P], U32, name="codes_late", tag="lower2", align_bytes=64)[:]
-        quantise(0, 3)
-        product_upper(3)
+        weave_pair(on_scalar, 1, 0, Q)
+        weave_group(on_vector, woven2_0[:], 1, 0)
+        weave_group(on_vector, woven2_rest[:, 0:GROUP], 1, 1)
+        quantise(1, 0, 1, woven2_0[:])
+        quantise(1, 1, 2, woven2_rest[:, 0:GROUP])
         for t in range(2):
-            copy_y1(t)
-        multiply_y12(0)
-        multiply_y12(1)
+            product(y2[t][:], 1, t, 0, V)
+        codes[0, 1] = keep.tile([P, 2 * P], U32, name="codes_late", tag="woven2_0", align_bytes=64)[:]
+        quantise(0, 2, 4, woven[0, 1])
+        quantise(1, 2, 4, woven[1, 1])
+        for t in range(2, 4):
+            product(y1_23[:, t - 2, :], 0, t, 0, V)
+        for t in range(2, 4):
+            for h in range(2):
+                product(y2_23[h][:, t - 2, :], 1, t, HALF * h, HALF * (h + 1))
+        for t in range(2):
+            nc.scalar.copy(y1_lower[:, t], y1_01[:, t, :])
+        multiply_lower(0)
 
-        weave_shared(2)
-        for t in range(4):
-            quantise(2, t)
+        for q0 in (0, Q // 2):
+            weave_pair(on_scalar, 2, q0, q0 + Q // 2)
+            weave_lower(on_vector, 2, q0, q0 + Q // 2)
+        multiply_lower(1)
+        quantise(2, 0, 2, woven[2, 0])
+        for t in range(2, 4):
+            quantise(2, t, t + 1, woven[2, 1][:, GROUP * (t - 2) : GROUP * (t - 1)])
         for h in range(2):
             v = slice(HALF * h, HALF * (h + 1))
-            nc.scalar.copy(y1_upper[:, :, v], y1_23[h][:])
-        for h in range(2):
-            y3.append(psum.tile([P, 4, HALF], F32, name="y3_%d" % h, tag="bank%d" % h))
-            for t in range(4):
-                product(y3[h][:, t, :], 2, t, HALF * h, HALF * (h + 1))
+            nc.scalar.copy(y1_upper[:, :, v], y1_23[:, :, v])
+        y3.append(psum.tile([P, 4, HALF], F32, name="y3_0", tag="bank0"))
+        for t in range(4):
+            product(y3[0][:, t, :], 2, t, 0, HALF)
         on_scalar(
             last_in[:, 0 : 4 * N].rearrange("p (c e t) -> p c t e", e=4, t=4),
-            raw4[:].rearrange("p t (c e) -> p c t e", e=4),
+            raw4[:].rearrange("p (t c e) -> p c t e", t=4, e=4),
         )
-        last_codes = keep.tile([P, N + V], U32, name="last_codes", tag="raw4", align_bytes=64)
+        last_codes = keep.tile([P, N + V], U32, name="last_codes", tag="raw4", align_bytes=DMA_ALIGN)
         multiply_upper(0)
+        y3.append(psum.tile([P, 4, HALF], F32, name="y3_1", tag="half0"))
+        for t in range(4):
+            product(y3[1][:, t, :], 2, t, HALF, V)
         multiply_upper(1)
         make_z(0)
         make_z(1)
@@ -226,4 +213,5 @@ def tile_picked_trilin_relu_p_kernel(tc, x_words, x_scales, w1, w2, w3, w4, offs
         last_product(0)
         quantise_last(N + HALF, N + V)
         last_product(1)
-        nc.scalar.dma_start(out, res[:])
+        for h in range(2):
+            nc.scalar.dma_start(out[:, HALF * h : HALF * (h + 1)], res[:, HALF * h : HALF * (h + 1)])

@@ -73,12 +73,12 @@ def tile_picked_trilin_relu_p_kernel(tc, x_words, x_scales, w1, w2, w3, w4, offs
             (0, 0): woven1[:, 0 : 2 * GROUP],
             (0, 1): woven1[:, 2 * GROUP : 4 * GROUP],
             (1, 1): woven2_rest[:, GROUP : 3 * GROUP],
-            (2, 0): raw[1][:, 0:H].bitcast(BF16),
+            (2, 0): woven2_rest[:, GROUP : 3 * GROUP],
             (2, 1): woven3_pair[:],
         }
         y12 = arena[:, 0 : 4 * H].rearrange("p (t c) -> p t c", t=4)[:, :, 0:V]
         y1_lower = raw[1].rearrange("p (t c) -> p t c", t=4)[:, 0:2, 0:V]
-        y1_upper = raw[2].rearrange("p (t c) -> p t c", t=4)[:, 0:2, V : 2 * V]
+        y1_upper = [raw[2][:, c0 : c0 + V].rearrange("p (t v) -> p t v", t=2) for c0 in (3 * H, V)]
 
         w_codes = [keep.tile([P, H], U32, name="w_codes%d" % d, align_bytes=64) for d in range(3)]
         w_sc = [keep.tile([P, H], U8, name="w_sc%d" % d, align_bytes=64) for d in range(3)]
@@ -129,7 +129,7 @@ def tile_picked_trilin_relu_p_kernel(tc, x_words, x_scales, w1, w2, w3, w4, offs
 
         def multiply_upper(h):
             v = slice(HALF * h, HALF * (h + 1))
-            nc.vector.tensor_tensor(y12[:, 2:4, v], y2_23[h][:], y1_upper[:, :, v], MULT)
+            nc.vector.tensor_tensor(y12[:, 2:4, v], y2_23[h][:], y1_upper[h], MULT)
 
         def make_z(h):
             nc.vector.tensor_tensor(
@@ -165,7 +165,8 @@ def tile_picked_trilin_relu_p_kernel(tc, x_words, x_scales, w1, w2, w3, w4, offs
         for t in range(2):
             product(y1_01[:, t, :], 0, t, 0, V)
 
-        weave_pair(on_scalar, 1, 0, Q)
+        for q0 in (0, Q // 2):
+            weave_pair(on_scalar, 1, q0, q0 + Q // 2)
         weave_group(on_vector, woven2_0[:], 1, 0)
         weave_group(on_vector, woven2_rest[:, 0:GROUP], 1, 1)
         quantise(1, 0, 1, woven2_0[:])
@@ -193,7 +194,7 @@ def tile_picked_trilin_relu_p_kernel(tc, x_words, x_scales, w1, w2, w3, w4, offs
             quantise(2, t, t + 1, woven[2, 1][:, GROUP * (t - 2) : GROUP * (t - 1)])
         for h in range(2):
             v = slice(HALF * h, HALF * (h + 1))
-            nc.scalar.copy(y1_upper[:, :, v], y1_23[:, :, v])
+            nc.scalar.copy(y1_upper[h], y1_23[:, :, v])
         y3.append(psum.tile([P, 4, HALF], F32, name="y3_0", tag="bank0"))
         for t in range(4):
             product(y3[0][:, t, :], 2, t, 0, HALF)

@@ -22,6 +22,7 @@ HALF = V // 2
 Q = H // 16
 LIST_COLS = V // 16
 CUT = 3 * H + H // 2
+Q_SCALAR = 28
 DMA_ALIGN = 256
 
 
@@ -76,18 +77,26 @@ def tile_picked_trilin_relu_p_kernel(tc, x_words, x_scales, w1, w2, w3, w4, offs
             (2, 0): woven2_rest[:, GROUP : 3 * GROUP],
             (2, 1): woven3_pair[:],
         }
-        y12 = arena[:, 0 : 4 * H].rearrange("p (t c) -> p t c", t=4)[:, :, 0:V]
-        y1_lower = raw[1].rearrange("p (t c) -> p t c", t=4)[:, 0:2, 0:V]
-        y1_upper = [raw[2][:, c0 : c0 + V].rearrange("p (t v) -> p t v", t=2) for c0 in (3 * H, V)]
+        y12 = arena[:, HALF : HALF + 4 * H].rearrange("p (t c) -> p t c", t=4)[:, :, 0:V]
+        y1_sbuf = [
+            raw[1][:, 0:V].rearrange("p (t v) -> p t v", t=1),
+            raw[1][:, H : H + HALF].rearrange("p (t v) -> p t v", t=1),
+            arena[:, H - HALF : H + HALF].rearrange("p (t v) -> p t v", t=2),
+            arena[:, 4 * H : 4 * H + 3 * HALF].rearrange("p (t v) -> p t v", t=3),
+        ]
 
         w_codes = [keep.tile([P, H], U32, name="w_codes%d" % d, align_bytes=64) for d in range(3)]
         w_sc = [keep.tile([P, H], U8, name="w_sc%d" % d, align_bytes=64) for d in range(3)]
         codes = {(d, u): w_codes[d][:, 2 * P * u : 2 * P * (u + 1)] for d in range(3) for u in range(2)}
 
-        y1_01 = psum.tile([P, 2, V], F32, name="y1_01", tag="bank0")
-        y1_23 = psum.tile([P, 2, V], F32, name="y1_23")
-        y2 = [psum.tile([P, V], F32, name="y2_%d" % t, tag="single%d" % t) for t in range(2)]
-        y2_23 = [psum.tile([P, 2, HALF], F32, name="y2_23_%d" % h, tag="half%d" % h) for h in range(2)]
+        parts = [(0, 1, 0, V), (1, 2, 0, HALF), (2, 4, 0, HALF), (1, 4, HALF, V)]
+        y1_head = psum.tile([P, V + HALF], F32, name="y1_head", tag="bank0")
+        y1 = [y1_head[:, 0:V].rearrange("p (t v) -> p t v", t=1), y1_head[:, V : V + HALF].rearrange("p (t v) -> p t v", t=1)]
+        y1 += [psum.tile([P, 2 + h, HALF], F32, name="y1_late%d" % h)[:] for h in range(2)]
+        y2 = [
+            psum.tile([P, t1 - t0, v1 - v0], F32, name="y2_%d" % n, tag="y2_%d" % n)[:]
+            for n, (t0, t1, v0, v1) in enumerate(parts)
+        ]
         y3 = []
 
         last_in = keep.tile([P, 4 * (N + V)], BF16, name="last_in", align_bytes=64)
@@ -124,12 +133,17 @@ def tile_picked_trilin_relu_p_kernel(tc, x_words, x_scales, w1, w2, w3, w4, offs
                 stop=True,
             )
 
-        def multiply_lower(t):
-            nc.vector.tensor_tensor(y12[:, t], y2[t][:], y1_lower[:, t], MULT)
+        def products(banks, d, t):
+            for n, (t0, t1, v0, v1) in enumerate(parts):
+                if t0 <= t < t1:
+                    product(banks[n][:, t - t0, :], d, t, v0, v1)
 
-        def multiply_upper(h):
-            v = slice(HALF * h, HALF * (h + 1))
-            nc.vector.tensor_tensor(y12[:, 2:4, v], y2_23[h][:], y1_upper[h], MULT)
+        def copy_y1(n):
+            nc.scalar.copy(y1_sbuf[n], y1[n])
+
+        def multiply(n):
+            t0, t1, v0, v1 = parts[n]
+            nc.vector.tensor_tensor(y12[:, t0:t1, v0:v1], y2[n], y1_sbuf[n], MULT)
 
         def make_z(h):
             nc.vector.tensor_tensor(
@@ -143,7 +157,7 @@ def tile_picked_trilin_relu_p_kernel(tc, x_words, x_scales, w1, w2, w3, w4, offs
             nc.vector.quantize_mx(last_codes[:, c0:c1].bitcast(FP8X4), last_sc[:, c0:c1], last_in[:, 4 * c0 : 4 * c1])
 
         def last_product(h):
-            acc = psum.tile([P, HALF], F32, name="acc%d" % h, tag="single%d" % h)
+            acc = psum.tile([P, HALF], F32, name="acc%d" % h, tag="y2_%d" % h)
             z_cols = slice(N + HALF * h, N + HALF * (h + 1))
             nc.tensor.matmul_mx(
                 acc[:],
@@ -163,7 +177,7 @@ def tile_picked_trilin_relu_p_kernel(tc, x_words, x_scales, w1, w2, w3, w4, offs
         weave_pair(on_scalar, 0, Q // 2, Q)
         quantise(0, 0, 2, woven[0, 0])
         for t in range(2):
-            product(y1_01[:, t, :], 0, t, 0, V)
+            products(y1, 0, t)
 
         for q0 in (0, Q // 2):
             weave_pair(on_scalar, 1, q0, q0 + Q // 2)
@@ -172,29 +186,29 @@ def tile_picked_trilin_relu_p_kernel(tc, x_words, x_scales, w1, w2, w3, w4, offs
         quantise(1, 0, 1, woven2_0[:])
         quantise(1, 1, 2, woven2_rest[:, 0:GROUP])
         for t in range(2):
-            product(y2[t][:], 1, t, 0, V)
+            products(y2, 1, t)
         codes[0, 1] = keep.tile([P, 2 * P], U32, name="codes_late", tag="woven2_0", align_bytes=64)[:]
         quantise(0, 2, 4, woven[0, 1])
         quantise(1, 2, 4, woven[1, 1])
         for t in range(2, 4):
-            product(y1_23[:, t - 2, :], 0, t, 0, V)
+            products(y1, 0, t)
         for t in range(2, 4):
-            for h in range(2):
-                product(y2_23[h][:, t - 2, :], 1, t, HALF * h, HALF * (h + 1))
-        for t in range(2):
-            nc.scalar.copy(y1_lower[:, t], y1_01[:, t, :])
-        multiply_lower(0)
+            products(y2, 1, t)
+        copy_y1(0)
+        copy_y1(1)
+        multiply(0)
 
+        weave_pair(on_scalar, 2, 0, Q // 2)
+        weave_pair(on_scalar, 2, Q // 2, Q_SCALAR)
         for q0 in (0, Q // 2):
-            weave_pair(on_scalar, 2, q0, q0 + Q // 2)
             weave_lower(on_vector, 2, q0, q0 + Q // 2)
-        multiply_lower(1)
+        weave_pair(on_vector, 2, Q_SCALAR, Q)
+        multiply(1)
         quantise(2, 0, 2, woven[2, 0])
         for t in range(2, 4):
             quantise(2, t, t + 1, woven[2, 1][:, GROUP * (t - 2) : GROUP * (t - 1)])
-        for h in range(2):
-            v = slice(HALF * h, HALF * (h + 1))
-            nc.scalar.copy(y1_upper[h], y1_23[:, :, v])
+        copy_y1(2)
+        copy_y1(3)
         y3.append(psum.tile([P, 4, HALF], F32, name="y3_0", tag="bank0"))
         for t in range(4):
             product(y3[0][:, t, :], 2, t, 0, HALF)
@@ -203,11 +217,11 @@ def tile_picked_trilin_relu_p_kernel(tc, x_words, x_scales, w1, w2, w3, w4, offs
             raw4[:].rearrange("p (t c e) -> p c t e", t=4, e=4),
         )
         last_codes = keep.tile([P, N + V], U32, name="last_codes", tag="raw4", align_bytes=DMA_ALIGN)
-        multiply_upper(0)
-        y3.append(psum.tile([P, 4, HALF], F32, name="y3_1", tag="half0"))
+        multiply(2)
+        y3.append(psum.tile([P, 4, HALF], F32, name="y3_1", tag="y2_2"))
         for t in range(4):
             product(y3[1][:, t, :], 2, t, HALF, V)
-        multiply_upper(1)
+        multiply(3)
         make_z(0)
         make_z(1)
         quantise_last(0, N + HALF)

from contextlib import ExitStack

import concourse.mybir as mybir

K, T, V, H, N = 512, 1024, 256, 512, 128
FLOPS = 2 * K * H * V * 3 + 2 * H * N * V

F32 = mybir.dt.float32
BF16 = mybir.dt.bfloat16
I32 = mybir.dt.int32
U32 = mybir.dt.uint32
U16 = mybir.dt.uint16
U8 = mybir.dt.uint8
FP8X4 = mybir.dt.float8_e4m3fn_x4
FP4X4 = mybir.dt.float4_e2m1fn_x4
MULT = mybir.AluOpType.mult
RELU = mybir.ActivationFunctionType.Relu

P = 128
GROUP = 4 * P
HALF = V // 2
Q = H // 16
LIST_COLS = V // 16
CUT = 3 * H + H // 2
Q_SCALAR = 28
DMA_ALIGN = 256


def tile_picked_trilin_relu_p_kernel(tc, x_words, x_scales, w1, w2, w3, w4, offs, out):
    nc = tc.nc
    with ExitStack() as ctx:
        keep = ctx.enter_context(tc.tile_pool(name="keep", bufs=1))
        psum = ctx.enter_context(tc.psum_pool(name="psum", bufs=1))

        scale_table = keep.tile([P, T], U8, name="scale_table", align_bytes=DMA_ALIGN)
        nc.vector.memset(scale_table[:].bitcast(I32), 0)
        word_table = keep.tile([P, T], U16, name="word_table", align_bytes=DMA_ALIGN)
        offsets = keep.tile([P, 3 * LIST_COLS], U16, name="offsets", align_bytes=DMA_ALIGN)
        nc.sync.dma_start(word_table[:].bitcast(I32), x_words[0].bitcast(I32))
        nc.sync.dma_start(offsets[:], offs)
        raw = [keep.tile([P, 4 * H], F32, name="raw%d" % d, align_bytes=DMA_ALIGN)[:] for d in range(2)]
        arena = keep.tile([P, 5 * H], F32, name="arena", align_bytes=DMA_ALIGN)
        raw.append(arena[:, H : 5 * H])
        rows = [w.rearrange("(p j) c -> p (j c)", j=4) for w in (w1, w2, w3)]
        nc.sync.dma_start(raw[0][:, 0 : 2 * H], rows[0][:, 0 : 2 * H])
        for quadrant in range(4):
            nc.sync.dma_start(
                scale_table[32 * quadrant : 32 * quadrant + 4, :].bitcast(I32),
                x_scales[0, 4 * quadrant : 4 * quadrant + 4, :].bitcast(I32),
            )
        nc.sync.dma_start(raw[0][:, 2 * H : 4 * H], rows[0][:, 2 * H : 4 * H])
        nc.sync.dma_start(raw[1], rows[1])
        for c0, c1 in ((0, CUT), (CUT, 4 * H)):
            nc.sync.dma_start(raw[2][:, c0:c1], rows[2][:, c0:c1])
        raw4 = keep.tile([P, 4 * N], F32, name="raw4", tag="raw4", align_bytes=DMA_ALIGN)
        for t in range(2):
            nc.sync.dma_start(raw4[:, N * t : N * (t + 1)], w4.rearrange("(q s r) n -> s q r n", s=4, r=4)[t])
        nc.sync.dma_start(raw4[:, 2 * N : 4 * N], w4.rearrange("(q u r e) n -> u q r (e n)", u=2, r=4, e=2)[1])

        words01 = keep.tile([P, 2 * V], U16, name="words01", align_bytes=64)
        words2 = keep.tile([P, V], U16, name="words2", align_bytes=64)
        picked_scales = keep.tile([P, 3 * V], U8, name="picked_scales", align_bytes=64)
        nc.vector.tensor_copy(words01[:], word_table[:].indirect(offsets[:, 0 : 2 * LIST_COLS]))
        nc.vector.tensor_copy(words2[:], word_table[:].indirect(offsets[:, 2 * LIST_COLS : 3 * LIST_COLS]))
        nc.vector.tensor_copy(picked_scales[:], scale_table[:].indirect(offsets[:]))
        x_codes = [words01[:, 0:V], words01[:, V : 2 * V], words2[:]]
        x_sc = [picked_scales[:, V * d : V * (d + 1)] for d in range(3)]

        woven1 = keep.tile([P, 4 * GROUP], BF16, name="woven1", align_bytes=64)
        woven2_0 = keep.tile([P, GROUP], BF16, name="woven2_0", tag="woven2_0", align_bytes=64)
        woven2_rest = keep.tile([P, 3 * GROUP], BF16, name="woven2_rest", align_bytes=64)
        woven3_pair = keep.tile([P, 2 * GROUP], BF16, name="woven3_pair", align_bytes=64)
        woven = {
            (0, 0): woven1[:, 0 : 2 * GROUP],
            (0, 1): woven1[:, 2 * GROUP : 4 * GROUP],
            (1, 1): woven2_rest[:, GROUP : 3 * GROUP],
            (2, 0): woven2_rest[:, GROUP : 3 * GROUP],
            (2, 1): woven3_pair[:],
        }
        y12 = arena[:, HALF : HALF + 4 * H].rearrange("p (t c) -> p t c", t=4)[:, :, 0:V]
        y1_sbuf = [
            raw[1][:, 0:V].rearrange("p (t v) -> p t v", t=1),
            raw[1][:, H : H + HALF].rearrange("p (t v) -> p t v", t=1),
            arena[:, H - HALF : H + HALF].rearrange("p (t v) -> p t v", t=2),
            arena[:, 4 * H : 4 * H + 3 * HALF].rearrange("p (t v) -> p t v", t=3),
        ]

        w_codes = [keep.tile([P, H], U32, name="w_codes%d" % d, align_bytes=64) for d in range(3)]
        w_sc = [keep.tile([P, H], U8, name="w_sc%d" % d, align_bytes=64) for d in range(3)]
        codes = {(d, u): w_codes[d][:, 2 * P * u : 2 * P * (u + 1)] for d in range(3) for u in range(2)}

        parts = [(0, 1, 0, V), (1, 2, 0, HALF), (2, 4, 0, HALF), (1, 4, HALF, V)]
        y1_head = psum.tile([P, V + HALF], F32, name="y1_head", tag="bank0")
        y1 = [y1_head[:, 0:V].rearrange("p (t v) -> p t v", t=1), y1_head[:, V : V + HALF].rearrange("p (t v) -> p t v", t=1)]
        y1 += [psum.tile([P, 2 + h, HALF], F32, name="y1_late%d" % h)[:] for h in range(2)]
        y2 = [
            psum.tile([P, t1 - t0, v1 - v0], F32, name="y2_%d" % n, tag="y2_%d" % n)[:]
            for n, (t0, t1, v0, v1) in enumerate(parts)
        ]
        y3 = []

        last_in = keep.tile([P, 4 * (N + V)], BF16, name="last_in", align_bytes=64)
        last_sc = keep.tile([P, N + V], U8, name="last_sc", align_bytes=64)
        res = keep.tile([P, V], F32, name="res", align_bytes=DMA_ALIGN)

        on_scalar, on_vector = nc.scalar.copy, nc.vector.tensor_copy

        def weave_group(copy, dst, d, t):
            src = raw[d].rearrange("p (j q s r) -> p s q j r", j=4, s=4, r=4)[:, t]
            copy(dst.rearrange("p (q r j) -> p q j r", r=4, j=4), src)

        def weave_lower(copy, d, q0, q1, j0=0, j1=4):
            src = raw[d].rearrange("p (j q s r) -> p s q j r", j=4, s=4, r=4)[:, 0:2, q0:q1, j0:j1]
            copy(woven[d, 0].rearrange("p (t q r j) -> p t q j r", t=2, r=4, j=4)[:, :, q0:q1, j0:j1], src)

        def weave_pair(copy, d, q0, q1, j0=0, j1=4):
            src = raw[d].rearrange("p (j q u h r e) -> p u q h j r e", j=4, u=2, h=2, r=2, e=2)[:, 1, q0:q1, :, j0:j1]
            dst = woven[d, 1].rearrange("p (e q h r j) -> p q h j r e", e=2, h=2, r=2, j=4)
            copy(dst[:, q0:q1, :, j0:j1], src)

        def quantise(d, t0, t1, src):
            u, c0, c1 = t0 // 2, P * (t0 % 2), P * (t1 - t0 + t0 % 2)
            nc.vector.quantize_mx(codes[d, u][:, c0:c1].bitcast(FP8X4), w_sc[d][:, P * t0 : P * t1], src)

        def product(bank, d, t, v0, v1):
            nc.tensor.matmul_mx(
                bank,
                lhsT=codes[d, t // 2][:, P * (t % 2) : P * (t % 2 + 1)].bitcast(FP8X4),
                lhsT_scale=w_sc[d][:, P * t : P * (t + 1)],
                rhs=x_codes[d][:, v0:v1].bitcast(FP4X4),
                rhs_scale=x_sc[d][:, v0:v1],
                start=True,
                stop=True,
            )

        def products(banks, d, t):
            for n, (t0, t1, v0, v1) in enumerate(parts):
                if t0 <= t < t1:
                    product(banks[n][:, t - t0, :], d, t, v0, v1)

        def copy_y1(n):
            nc.scalar.copy(y1_sbuf[n], y1[n])

        def multiply(n):
            t0, t1, v0, v1 = parts[n]
            nc.vector.tensor_tensor(y12[:, t0:t1, v0:v1], y2[n], y1_sbuf[n], MULT)

        def make_z(h):
            nc.vector.tensor_tensor(
                last_in[:, 4 * (N + HALF * h) : 4 * (N + HALF * (h + 1))].rearrange("p (c e t) -> p c t e", e=4, t=4),
                y3[h][:].rearrange("p t (c e) -> p c t e", e=4),
                y12[:, :, HALF * h : HALF * (h + 1)].rearrange("p t (c e) -> p c t e", e=4),
                MULT,
            )

        def quantise_last(c0, c1):
            nc.vector.quantize_mx(last_codes[:, c0:c1].bitcast(FP8X4), last_sc[:, c0:c1], last_in[:, 4 * c0 : 4 * c1])

        def last_product(h):
            acc = psum.tile([P, HALF], F32, name="acc%d" % h, tag="y2_%d" % h)
            z_cols = slice(N + HALF * h, N + HALF * (h + 1))
            nc.tensor.matmul_mx(
                acc[:],
                lhsT=last_codes[:, 0:N].bitcast(FP8X4),
                lhsT_scale=last_sc[:, 0:N],
                rhs=last_codes[:, z_cols].bitcast(FP8X4),
                rhs_scale=last_sc[:, z_cols],
                start=True,
                stop=True,
            )
            nc.scalar.activation(res[:, HALF * h : HALF * (h + 1)], acc[:], RELU)

        weave_lower(on_scalar, 0, 0, Q, 0, 2)
        weave_pair(on_scalar, 0, 0, Q // 2, 0, 2)
        weave_lower(on_scalar, 0, 0, Q, 2, 4)
        weave_pair(on_scalar, 0, 0, Q // 2, 2, 4)
        weave_pair(on_scalar, 0, Q // 2, Q)
        quantise(0, 0, 2, woven[0, 0])
        for t in range(2):
            products(y1, 0, t)

        for q0 in (0, Q // 2):
            weave_pair(on_scalar, 1, q0, q0 + Q // 2)
        weave_group(on_vector, woven2_0[:], 1, 0)
        weave_group(on_vector, woven2_rest[:, 0:GROUP], 1, 1)
        quantise(1, 0, 1, woven2_0[:])
        quantise(1, 1, 2, woven2_rest[:, 0:GROUP])
        for t in range(2):
            products(y2, 1, t)
        codes[0, 1] = keep.tile([P, 2 * P], U32, name="codes_late", tag="woven2_0", align_bytes=64)[:]
        quantise(0, 2, 4, woven[0, 1])
        quantise(1, 2, 4, woven[1, 1])
        for t in range(2, 4):
            products(y1, 0, t)
        for t in range(2, 4):
            products(y2, 1, t)
        copy_y1(0)
        copy_y1(1)
        multiply(0)

        weave_pair(on_scalar, 2, 0, Q // 2)
        weave_pair(on_scalar, 2, Q // 2, Q_SCALAR)
        for q0 in (0, Q // 2):
            weave_lower(on_vector, 2, q0, q0 + Q // 2)
        weave_pair(on_vector, 2, Q_SCALAR, Q)
        multiply(1)
        quantise(2, 0, 2, woven[2, 0])
        for t in range(2, 4):
            quantise(2, t, t + 1, woven[2, 1][:, GROUP * (t - 2) : GROUP * (t - 1)])
        copy_y1(2)
        copy_y1(3)
        y3.append(psum.tile([P, 4, HALF], F32, name="y3_0", tag="bank0"))
        for t in range(4):
            product(y3[0][:, t, :], 2, t, 0, HALF)
        on_scalar(
            last_in[:, 0 : 4 * N].rearrange("p (c e t) -> p c t e", e=4, t=4),
            raw4[:].rearrange("p (t c e) -> p c t e", t=4, e=4),
        )
        last_codes = keep.tile([P, N + V], U32, name="last_codes", tag="raw4", align_bytes=DMA_ALIGN)
        multiply(2)
        y3.append(psum.tile([P, 4, HALF], F32, name="y3_1", tag="y2_2"))
        for t in range(4):
            product(y3[1][:, t, :], 2, t, HALF, V)
        multiply(3)
        make_z(0)
        make_z(1)
        quantise_last(0, N + HALF)
        last_product(0)
        quantise_last(N + HALF, N + V)
        last_product(1)
        for h in range(2):
            nc.scalar.dma_start(out[:, HALF * h : HALF * (h + 1)], res[:, HALF * h : HALF * (h + 1)])
